import numpy as np
import ml_dtypes


def mxq(x, axis, fmt="e4m3"):
    dtype, down = {"e4m3": (ml_dtypes.float8_e4m3fn, 7), "e5m2": (ml_dtypes.float8_e5m2, 14)}[fmt]
    v = np.moveaxis(np.asarray(x, np.float32).astype(ml_dtypes.bfloat16).astype(np.float64), axis, -1)
    blocks = v.reshape(v.shape[:-1] + (-1, 32))
    amax = np.abs(blocks).max(-1, keepdims=True)
    byte = np.maximum(np.where(amax > 0, np.frexp(amax)[1] - 1 + 127, 0) - down, 1)
    scale = np.exp2(byte - 127.0)
    codes = (blocks / scale).astype(np.float32).astype(dtype).astype(np.float64)
    return np.moveaxis((codes * scale).reshape(v.shape), -1, axis)


WIDE = False


def mx_kscale(k):
    if not WIDE:
        return np.ones(k)
    levels = np.array([24, -24, 12, -12, 0])
    if k % 512:
        return np.exp2(np.random.permutation(np.resize(levels, k // 32))).repeat(32)
    a = np.empty((k // 512, 16))
    for p in range(k // 512):
        a[p, :8] = np.random.permutation(np.resize(levels, 8))
        for g in range(8):
            far = levels[np.abs(levels - a[p, g]) >= 10]
            a[p, g + 8] = far[np.random.randint(len(far))]
    return np.exp2(a.ravel()).repeat(32)


def f64(x):
    return np.asarray(x).astype(np.float64)


def striped8(idx):
    return np.concatenate([v.reshape(-1, 16).T for v in idx]).astype(np.uint16)


def unstriped8(offs):
    return np.stack([offs[16 * g:16 * g + 16].T.reshape(-1) for g in range(8)]).astype(np.int64)


E2M1 = np.array([0.0, 0.5, 1.0, 1.5, 2.0, 3.0, 4.0, 6.0, -0.0, -0.5, -1.0, -1.5, -2.0, -3.0, -4.0, -6.0])


def pack_weight(w, fmt):
    k, n = w.shape
    w = f64(np.asarray(w, np.float32).astype(ml_dtypes.bfloat16)).reshape(k // 32, 32, n)
    amax = np.abs(w).max(1)
    if fmt == "e4m3":
        byte = np.frexp(amax)[1] - 1 + 127 - 7
    else:
        mant, ex = np.frexp(amax / 6.0)
        byte = np.where(mant > 0.5, ex, ex - 1) + 127
    byte = np.clip(np.where(amax > 0, byte, 1), 1, 254)
    scaled = (w * np.exp2(127.0 - byte)[:, None, :]).reshape(k, n).astype(np.float32)
    by_word = np.ascontiguousarray(scaled.reshape(k // 512, 128, 4, n).transpose(0, 1, 3, 2))
    if fmt == "e4m3":
        words = by_word.astype(ml_dtypes.float8_e4m3fn).view(np.uint8)
    else:
        c = by_word.astype(ml_dtypes.float4_e2m1fn).view(np.uint8) & 0xF
        words = (c[..., 0::2] | (c[..., 1::2] << 4)).reshape(k // 512, 128, 2 * n)
    return np.ascontiguousarray(words), np.ascontiguousarray(byte.astype(np.uint8).reshape(k // 512, 16, n))


def unpack_weight(words, scales, fmt):
    g, _, n = scales.shape
    words = np.ascontiguousarray(words).reshape(g, 128, n, -1)
    if fmt == "e4m3":
        vals = words.view(ml_dtypes.float8_e4m3fn).astype(np.float64)
    else:
        nib = np.empty((g, 128, n, 4), np.uint8)
        nib[..., 0::2] = words & 0xF
        nib[..., 1::2] = words >> 4
        vals = E2M1[nib]
    vals = vals * np.repeat(np.exp2(scales.astype(np.float64) - 127.0), 8, axis=1)[..., None]
    return vals.transpose(0, 1, 3, 2).reshape(g * 512, n)


K, R, N, T, J = 1024, 512, 512, 2048, 1024


def setup_inputs():
    n = np.random.standard_normal
    s = mx_kscale(K)[:, None]
    u = mx_kscale(R)[:, None]
    p_wg = pack_weight(n((K, R)) / np.sqrt(K) / s, "e2m1")
    return {
        "xT": (n((K, T)) * s).astype(np.float32),
        "wgt": np.repeat(np.random.uniform(0.5, 2.0, (8, J)), 16, axis=0).astype(np.float32),
        "wg_words": p_wg[0],
        "wg_scales": p_wg[1],
        "wu": (n((K, R)) / np.sqrt(K) / s * u.T).astype(np.float32),
        "wd": (n((R, N)) / np.sqrt(R) / u).astype(np.float32),
        "b": (0.3 * n(N)).astype(np.float32),
        "offs": striped8(np.stack([np.random.permutation(T)[:J] for _ in range(8)])),
    }


def reference(xT, wgt, wg_words, wg_scales, wu, wd, b, offs):
    idx = unstriped8(offs)
    rows = np.arange(K)
    xg = f64(wgt)[rows // 4 % 128] * f64(xT)[rows[:, None], idx[rows % 512 // 64]]
    xT_ = mxq(xg, 0, "e4m3")
    wg_ = unpack_weight(wg_words, wg_scales, "e2m1")
    wu_ = mxq(f64(wu), 0, "e4m3")
    ga = wg_.T @ xT_
    ub = wu_.T @ xT_
    h = np.tanh(ga) * ub
    h_ = mxq(h, 0, "e4m3")
    wd_ = mxq(f64(wd), 0, "e4m3")
    y = wd_.T @ h_
    return y + f64(b)[:, None]

@@ -1,0 +1,233 @@
+from contextlib import ExitStack
+
+import concourse.mybir as mybir
+
+K, R, N, T, J = 1024, 512, 512, 2048, 1024
+FLOPS = 2 * J * (2 * K * R + R * N)
+
+F32 = mybir.dt.float32
+BF16 = mybir.dt.bfloat16
+I32 = mybir.dt.int32
+U32 = mybir.dt.uint32
+U16 = mybir.dt.uint16
+U8 = mybir.dt.uint8
+FP8X4 = mybir.dt.float8_e4m3fn_x4
+FP4X4 = mybir.dt.float4_e2m1fn_x4
+ACT = mybir.ActivationFunctionType
+MULT = mybir.AluOpType.mult
+
+P = 128
+PACK = 4
+KP = P * PACK
+PASSES = K // KP
+HALF = 512
+QUART = 256
+CH = 128
+
+
+def tile_list_tanh_bias_kernel(tc, xT, wgt, wg_words, wg_scales, wu, wd, b, offs, out):
+    nc = tc.nc
+    with ExitStack() as ctx:
+        sb = ctx.enter_context(tc.tile_pool(name="sb", bufs=1))
+        ps = ctx.enter_context(tc.psum_pool(name="ps", bufs=8))
+
+        def tile(name, shape, dtype):
+            return sb.tile(shape, dtype, name=name, align_bytes=64)
+
+        offsets = sb.tile([P, J // 16], U16, name="offsets")
+        wg_raw = tile("wg_raw", [P, PASSES, 2 * R], U8)
+        sg_raw = tile("sg_raw", [P, PASSES, R], U8)
+        wg_c = tile("wg_c", [P, PASSES, PACK, 2 * P], U8)
+        wg_s = tile("wg_s", [P, PASSES, PACK, P], U8)
+        wgt_sb = [tile("wgt%d" % h, [P, HALF], F32) for h in range(2)]
+        x_sb = [[tile("x%d%d" % (a, i), [P, T], F32) for i in range(PACK)] for a in range(PASSES)]
+        wu_raw = tile("wu_raw", [P, PASSES, PACK, R], F32)
+        wd_raw = tile("wd_raw", [P, PACK, N], F32)
+        bias = tile("bias", [P, PACK], F32)
+        warm = tile("warm", [P, 16], F32)
+
+        nc.vector.memset(sg_raw[:].rearrange("p a r -> p (a r)").bitcast(I32), 0)
+        nc.vector.memset(warm[:, 0:8], 0.0)
+        nc.sync.dma_start(offsets[:], offs)
+        nc.sync.dma_start(out=wg_raw[:].bitcast(I32), in_=wg_words.rearrange("a p n -> p a n").bitcast(I32))
+        nc.sync.dma_start(out=wgt_sb[0][:], in_=wgt[:, 0:HALF])
+        for q in range(4):
+            nc.scalar.dma_start(
+                out=sg_raw[32 * q : 32 * q + 4, :, :].bitcast(I32),
+                in_=wg_scales[:, 4 * q : 4 * q + 4, :].rearrange("a r n -> r a n").bitcast(I32),
+            )
+        nc.scalar.dma_start(out=bias[:], in_=b.rearrange("(p c) -> p c", c=PACK))
+        nc.scalar.activation(out=warm[:, 8:16], in_=warm[:, 0:8], func=ACT.Tanh)
+        for a in range(PASSES):
+            rows = xT[a * KP : (a + 1) * KP, :].rearrange("(p i) t -> p i t", i=PACK)
+            for i in range(PACK):
+                nc.sync.dma_start(out=x_sb[a][i][:], in_=rows[:, i, :])
+                if a == 0 and i == 0:
+                    nc.sync.dma_start(out=wgt_sb[1][:], in_=wgt[:, HALF:J])
+        for a in range(PASSES):
+            nc.sync.dma_start(out=wu_raw[:, a, :, :], in_=wu[a * KP : (a + 1) * KP, :].rearrange("(p i) r -> p i r", i=PACK))
+        nc.sync.dma_start(out=wd_raw[:], in_=wd.rearrange("(p i) n -> p i n", i=PACK))
+
+        nc.vector.tensor_copy(
+            out=wg_c[:].bitcast(U16).rearrange("p a t m -> p a m t"),
+            in_=wg_raw[:].bitcast(U16).rearrange("p a (m t) -> p a m t", t=PACK),
+        )
+        nc.vector.tensor_copy(
+            out=wg_s[:].rearrange("p a t m -> p a m t"),
+            in_=sg_raw[:].rearrange("p a (m t) -> p a m t", t=PACK),
+        )
+
+        g = [[tile("g%d%d" % (a, h), [P, PACK, HALF], F32) for h in range(2)] for a in range(PASSES)]
+        stage = tile("stage", [P, 2, PASSES, HALF, PACK], BF16)
+        xbh = [[stage[:, h, a, :, :] for h in range(2)] for a in range(PASSES)]
+        xb = [[xbh[a][q // 2][:, (q % 2) * QUART : (q % 2 + 1) * QUART, :] for q in range(4)] for a in range(PASSES)]
+        xc = [tile("xc%d" % a, [P, J], U32) for a in range(PASSES)]
+        xs = [tile("xs%d" % a, [P, J], U8) for a in range(PASSES)]
+
+        def gather(a, i, j0, w):
+            h, c0 = divmod(j0, HALF)
+            nc.vector.tensor_tensor(
+                g[a][h][:, i, c0 : c0 + w],
+                x_sb[a][i][:].indirect(offsets[:, j0 // 16 : (j0 + w) // 16]),
+                wgt_sb[h][:, c0 : c0 + w],
+                MULT,
+            )
+
+        def interleave_x(a, q):
+            h, c0 = divmod(q * QUART, HALF)
+            nc.scalar.copy(
+                out=xb[a][q].rearrange("p (c i) t -> p c t i", i=4),
+                in_=g[a][h][:, :, c0 : c0 + QUART].rearrange("p t (c i) -> p c t i", i=4),
+            )
+
+        def quantize(codes, scales, src):
+            nc.vector.quantize_mx(out=codes.bitcast(FP8X4), scales=scales, in_=src)
+
+        def quantize_x(a, q):
+            cols = slice(q * QUART, (q + 1) * QUART)
+            quantize(xc[a][:, cols], xs[a][:, cols], xb[a][q].rearrange("p j t -> p (j t)"))
+
+        def weight_views(raw, dst):
+            return dst.rearrange("p t m i -> p m i t"), raw[:].rearrange("p i (m t) -> p m i t", t=PACK)
+
+        for i in range(PACK):
+            for h in range(2):
+                gather(0, i, h * HALF, HALF)
+        for q in range(4):
+            interleave_x(0, q)
+        for i in range(PACK - 1):
+            for h in range(2):
+                gather(1, i, h * HALF, HALF)
+            if i >= 1:
+                quantize_x(0, 2 * (i - 1))
+                quantize_x(0, 2 * (i - 1) + 1)
+        for q in range(4):
+            gather(1, PACK - 1, q * QUART, QUART)
+            interleave_x(1, q)
+            if q in (1, 2):
+                quantize_x(1, q - 1)
+
+        wu_c = [tile("wu_c%d" % a, [P, R], U32) for a in range(PASSES)]
+        wu_s = [tile("wu_s%d" % a, [P, R], U8) for a in range(PASSES)]
+        nc.vector.tensor_copy(
+            out=stage[:, 0, :, :, :].rearrange("p a (t m) i -> p a m i t", t=PACK),
+            in_=wu_raw[:].rearrange("p a i (m t) -> p a m i t", t=PACK),
+        )
+        quantize_x(1, 2)
+        for a in range(PASSES):
+            quantize(wu_c[a][:], wu_s[a][:], xbh[a][0].rearrange("p j t -> p (j t)"))
+        quantize_x(1, 3)
+
+        wd_b = xbh[0][1].rearrange("p (t m) i -> p t m i", t=PACK)
+        wd_c = tile("wd_c", [P, N], U32)
+        wd_s = tile("wd_s", [P, N], U8)
+
+        tg = [tile("tg%d" % h, [P, PACK, HALF], F32) for h in range(2)]
+        hb = [tile("hb%d" % q, [P, QUART, PACK], BF16) for q in range(4)]
+        hc = [tile("hc%d" % q, [P, QUART], U32) for q in range(4)]
+        hs = [tile("hs%d" % q, [P, QUART], U8) for q in range(4)]
+        o_sb = [[tile("o%d%d" % (q, u), [P, 2, QUART], F32) for u in range(2)] for q in range(4)]
+        out_v = out.rearrange("(p c) j -> p c j", c=PACK)
+
+        ga = [[ps.tile([P, HALF], F32, name="ga%d%d" % (h, t), tag="bank") for t in range(PACK)] for h in range(2)]
+
+        def gate(h, a):
+            cols = slice(h * HALF, (h + 1) * HALF)
+            for t in range(PACK):
+                nc.tensor.matmul_mx(
+                    out=ga[h][t][:],
+                    lhsT=wg_c[:, a, t, :].bitcast(FP4X4),
+                    lhsT_scale=wg_s[:, a, t, :],
+                    rhs=xc[a][:, cols].bitcast(FP8X4),
+                    rhs_scale=xs[a][:, cols],
+                    start=(a == 0),
+                    stop=(a == PASSES - 1),
+                )
+
+        def gate_tanh(h):
+            for t in range(PACK):
+                nc.scalar.activation(out=tg[h][:, t, :], in_=ga[h][t][:], func=ACT.Tanh)
+
+        def up(c):
+            q, c0 = divmod(c * CH, QUART)
+            h, h0 = divmod(c * CH, HALF)
+            cols = slice(c * CH, (c + 1) * CH)
+            acc = ps.tile([P, PACK, CH], F32, name="ub", tag="bank")
+            for t in range(PACK):
+                for a in range(PASSES):
+                    nc.tensor.matmul_mx(
+                        out=acc[:, t, :],
+                        lhsT=wu_c[a][:, t * P : (t + 1) * P].bitcast(FP8X4),
+                        lhsT_scale=wu_s[a][:, t * P : (t + 1) * P],
+                        rhs=xc[a][:, cols].bitcast(FP8X4),
+                        rhs_scale=xs[a][:, cols],
+                        start=(a == 0),
+                        stop=(a == PASSES - 1),
+                    )
+            nc.vector.tensor_tensor(
+                hb[q][:, c0 : c0 + CH, :].rearrange("p (c i) t -> p c t i", i=4),
+                acc[:].rearrange("p t (c i) -> p c t i", i=4),
+                tg[h][:, :, h0 : h0 + CH].rearrange("p t (c i) -> p c t i", i=4),
+                MULT,
+            )
+
+        def down(q):
+            for u in range(2):
+                acc = ps.tile([P, 2, QUART], F32, name="y", tag="bank")
+                for v in range(2):
+                    c = 2 * u + v
+                    nc.tensor.matmul_mx(
+                        out=acc[:, v, :],
+                        lhsT=wd_c[:, c * P : (c + 1) * P].bitcast(FP8X4),
+                        lhsT_scale=wd_s[:, c * P : (c + 1) * P],
+                        rhs=hc[q][:].bitcast(FP8X4),
+                        rhs_scale=hs[q][:],
+                        start=True,
+                        stop=True,
+                    )
+                for v in range(2):
+                    c = 2 * u + v
+                    if q == 3 and u == 1:
+                        nc.vector.tensor_scalar_add(o_sb[q][u][:, v, :], acc[:, v, :], bias[:, c : c + 1])
+                    else:
+                        nc.scalar.activation(out=o_sb[q][u][:, v, :], in_=acc[:, v, :], func=ACT.Identity, bias=bias[:, c : c + 1])
+                nc.sync.dma_start(out=out_v[:, 2 * u : 2 * u + 2, q * QUART : (q + 1) * QUART], in_=o_sb[q][u][:])
+
+        for a in range(PASSES):
+            for h in range(2):
+                gate(h, a)
+        gate_tanh(0)
+        o, s = weight_views(wd_raw, wd_b)
+        nc.scalar.copy(out=o[:, 0:64], in_=s[:, 0:64])
+        gate_tanh(1)
+        for q in range(4):
+            up(2 * q)
+            up(2 * q + 1)
+            if q == 0:
+                nc.vector.tensor_copy(out=o[:, 64:128], in_=s[:, 64:128])
+            quantize(hc[q][:], hs[q][:], hb[q][:].rearrange("p j t -> p (j t)"))
+            if q == 0:
+                quantize(wd_c[:], wd_s[:], wd_b.rearrange("p t m i -> p (t m i)"))
+            else:
+                down(q - 1)
+        down(3)

@@ -23,13 +23,14 @@ PASSES = K // KP
 HALF = 512
 QUART = 256
 CH = 128
+GROUPS = [(0, 256), (256, 256), (512, 256), (768, 128), (896, 128)]
 
 
 def tile_list_tanh_bias_kernel(tc, xT, wgt, wg_words, wg_scales, wu, wd, b, offs, out):
     nc = tc.nc
     with ExitStack() as ctx:
         sb = ctx.enter_context(tc.tile_pool(name="sb", bufs=1))
-        ps = ctx.enter_context(tc.psum_pool(name="ps", bufs=8))
+        ps = [ctx.enter_context(tc.psum_pool(name="ps%d" % h, bufs=PACK)) for h in range(2)]
 
         def tile(name, shape, dtype):
             return sb.tile(shape, dtype, name=name, align_bytes=64)
@@ -39,7 +40,8 @@ def tile_list_tanh_bias_kernel(tc, xT, wgt, wg_words, wg_scales, wu, wd, b, offs
         sg_raw = tile("sg_raw", [P, PASSES, R], U8)
         wg_c = tile("wg_c", [P, PASSES, PACK, 2 * P], U8)
         wg_s = tile("wg_s", [P, PASSES, PACK, P], U8)
-        wgt_sb = [tile("wgt%d" % h, [P, HALF], F32) for h in range(2)]
+        g1 = tile("g1", [P, PACK + 2, HALF], F32)
+        wgt_sb = [g1[:, 1, :], tile("wgt1", [P, HALF], F32)[:]]
         x_sb = [[tile("x%d%d" % (a, i), [P, T], F32) for i in range(PACK)] for a in range(PASSES)]
         wu_raw = tile("wu_raw", [P, PASSES, PACK, R], F32)
         wd_raw = tile("wd_raw", [P, PACK, N], F32)
@@ -50,37 +52,42 @@ def tile_list_tanh_bias_kernel(tc, xT, wgt, wg_words, wg_scales, wu, wd, b, offs
         nc.vector.memset(warm[:, 0:8], 0.0)
         nc.sync.dma_start(offsets[:], offs)
         nc.sync.dma_start(out=wg_raw[:].bitcast(I32), in_=wg_words.rearrange("a p n -> p a n").bitcast(I32))
-        nc.sync.dma_start(out=wgt_sb[0][:], in_=wgt[:, 0:HALF])
+        nc.sync.dma_start(out=wgt_sb[0], in_=wgt[:, 0:HALF])
         for q in range(4):
-            nc.scalar.dma_start(
+            nc.sync.dma_start(
                 out=sg_raw[32 * q : 32 * q + 4, :, :].bitcast(I32),
                 in_=wg_scales[:, 4 * q : 4 * q + 4, :].rearrange("a r n -> r a n").bitcast(I32),
             )
-        nc.scalar.dma_start(out=bias[:], in_=b.rearrange("(p c) -> p c", c=PACK))
         nc.scalar.activation(out=warm[:, 8:16], in_=warm[:, 0:8], func=ACT.Tanh)
-        for a in range(PASSES):
+
+        def load_x(plane):
+            a, i = divmod(plane, PACK)
             rows = xT[a * KP : (a + 1) * KP, :].rearrange("(p i) t -> p i t", i=PACK)
-            for i in range(PACK):
-                nc.sync.dma_start(out=x_sb[a][i][:], in_=rows[:, i, :])
-                if a == 0 and i == 0:
-                    nc.sync.dma_start(out=wgt_sb[1][:], in_=wgt[:, HALF:J])
-        for a in range(PASSES):
+            nc.sync.dma_start(out=x_sb[a][i][:], in_=rows[:, i, :])
+
+        def load_wu(a):
             nc.sync.dma_start(out=wu_raw[:, a, :, :], in_=wu[a * KP : (a + 1) * KP, :].rearrange("(p i) r -> p i r", i=PACK))
+
+        load_x(0)
+        nc.sync.dma_start(out=wgt_sb[1], in_=wgt[:, HALF:J])
+        for plane in range(1, 8):
+            load_x(plane)
+        load_wu(0)
+        load_wu(1)
         nc.sync.dma_start(out=wd_raw[:], in_=wd.rearrange("(p i) n -> p i n", i=PACK))
+        nc.sync.dma_start(out=bias[:], in_=b.rearrange("(p c) -> p c", c=PACK))
 
         nc.vector.tensor_copy(
-            out=wg_c[:].bitcast(U16).rearrange("p a t m -> p a m t"),
-            in_=wg_raw[:].bitcast(U16).rearrange("p a (m t) -> p a m t", t=PACK),
+            out=wg_c[:].bitcast(U16),
+            in_=wg_raw[:].bitcast(U16).rearrange("p a (m t) -> p a t m", t=PACK),
         )
         nc.vector.tensor_copy(
-            out=wg_s[:].rearrange("p a t m -> p a m t"),
-            in_=sg_raw[:].rearrange("p a (m t) -> p a m t", t=PACK),
+            out=wg_s[:],
+            in_=sg_raw[:].rearrange("p a (m t) -> p a t m", t=PACK),
         )
 
-        g = [[tile("g%d%d" % (a, h), [P, PACK, HALF], F32) for h in range(2)] for a in range(PASSES)]
-        stage = tile("stage", [P, 2, PASSES, HALF, PACK], BF16)
-        xbh = [[stage[:, h, a, :, :] for h in range(2)] for a in range(PASSES)]
-        xb = [[xbh[a][q // 2][:, (q % 2) * QUART : (q % 2 + 1) * QUART, :] for q in range(4)] for a in range(PASSES)]
+        g = [[tile("g0%d" % h, [P, PACK, HALF], F32)[:] for h in range(2)], [g1[:, 2 : PACK + 2, :], g1[:, 0:PACK, :]]]
+        xbh = [[tile("xb%d%d" % (a, h), [P, HALF, PACK], BF16)[:] for h in range(2)] for a in range(PASSES)]
         xc = [tile("xc%d" % a, [P, J], U32) for a in range(PASSES)]
         xs = [tile("xs%d" % a, [P, J], U8) for a in range(PASSES)]
 
@@ -93,63 +100,73 @@ def tile_list_tanh_bias_kernel(tc, xT, wgt, wg_words, wg_scales, wu, wd, b, offs
                 MULT,
             )
 
-        def interleave_x(a, q):
-            h, c0 = divmod(q * QUART, HALF)
-            nc.scalar.copy(
-                out=xb[a][q].rearrange("p (c i) t -> p c t i", i=4),
-                in_=g[a][h][:, :, c0 : c0 + QUART].rearrange("p t (c i) -> p c t i", i=4),
+        def interleave_x(copy, a, j0, w):
+            h, c0 = divmod(j0, HALF)
+            copy(
+                out=xbh[a][h][:, c0 : c0 + w, :].rearrange("p (c i) t -> p c t i", i=4),
+                in_=g[a][h][:, :, c0 : c0 + w].rearrange("p t (c i) -> p c t i", i=4),
             )
 
         def quantize(codes, scales, src):
             nc.vector.quantize_mx(out=codes.bitcast(FP8X4), scales=scales, in_=src)
 
-        def quantize_x(a, q):
-            cols = slice(q * QUART, (q + 1) * QUART)
-            quantize(xc[a][:, cols], xs[a][:, cols], xb[a][q].rearrange("p j t -> p (j t)"))
+        def quantize_x(a, j0, w):
+            h, c0 = divmod(j0, HALF)
+            cols = slice(j0, j0 + w)
+            quantize(xc[a][:, cols], xs[a][:, cols], xbh[a][h][:, c0 : c0 + w, :].rearrange("p j t -> p (j t)"))
 
-        def weight_views(raw, dst):
-            return dst.rearrange("p t m i -> p m i t"), raw[:].rearrange("p i (m t) -> p m i t", t=PACK)
+        def interleave_w(copy, raw, dst, m0=0, m1=P):
+            copy(out=dst.rearrange("p t m i -> p m i t")[:, m0:m1], in_=raw.rearrange("p i (m t) -> p m i t", t=PACK)[:, m0:m1])
+
+        g1_tail = g1[:].rearrange("p s j -> p (s j)")[:, 3 * HALF + QUART : 5 * HALF + QUART].bitcast(BF16)
+        wu_b = [tile("wu_b0", [P, PACK, P, PACK], BF16)[:], g1_tail.rearrange("p (t m i) -> p t m i", t=PACK, i=PACK)]
+        wu_c = [tile("wu_c%d" % a, [P, R], U32) for a in range(PASSES)]
+        wu_s = [tile("wu_s%d" % a, [P, R], U8) for a in range(PASSES)]
+        wd_b = tile("wd_b", [P, PACK, P, PACK], BF16)[:]
+
+        def quantize_wu(a):
+            quantize(wu_c[a][:], wu_s[a][:], wu_b[a].rearrange("p t m i -> p (t m i)"))
 
         for i in range(PACK):
             for h in range(2):
                 gather(0, i, h * HALF, HALF)
-        for q in range(4):
-            interleave_x(0, q)
-        for i in range(PACK - 1):
-            for h in range(2):
-                gather(1, i, h * HALF, HALF)
-            if i >= 1:
-                quantize_x(0, 2 * (i - 1))
-                quantize_x(0, 2 * (i - 1) + 1)
-        for q in range(4):
-            gather(1, PACK - 1, q * QUART, QUART)
-            interleave_x(1, q)
-            if q in (1, 2):
-                quantize_x(1, q - 1)
+        for h in range(2):
+            interleave_x(nc.scalar.copy, 0, h * HALF, HALF)
+        gather(1, 0, 0, HALF)
+        gather(1, 0, HALF, HALF)
+        gather(1, 1, 0, HALF)
+        quantize_x(0, 0, HALF)
+        gather(1, 2, 0, HALF)
+        quantize_x(0, HALF, HALF)
+        for q in range(2):
+            gather(1, 3, q * QUART, QUART)
+            interleave_x(nc.scalar.copy, 1, q * QUART, QUART)
+        interleave_w(nc.scalar.copy, wu_raw[:, 0, :, :], wu_b[0])
+        interleave_w(nc.scalar.copy, wu_raw[:, 1, :, :], wu_b[1], 0, P // 2)
+        gather(1, 1, HALF, HALF)
+        quantize_x(1, 0, HALF)
+        gather(1, 2, HALF, HALF)
+        interleave_w(nc.vector.tensor_copy, wu_raw[:, 1, :, :], wu_b[1], P // 2, P)
+        quantize_wu(0)
+        gather(1, 3, 2 * QUART, QUART)
+        quantize_wu(1)
+        gather(1, 3, 3 * QUART, QUART)
+        for q in range(2, 4):
+            interleave_x(nc.vector.tensor_copy, 1, q * QUART, QUART)
+        for q in range(2, 4):
+            quantize_x(1, q * QUART, QUART)
 
-        wu_c = [tile("wu_c%d" % a, [P, R], U32) for a in range(PASSES)]
-        wu_s = [tile("wu_s%d" % a, [P, R], U8) for a in range(PASSES)]
-        nc.vector.tensor_copy(
-            out=stage[:, 0, :, :, :].rearrange("p a (t m) i -> p a m i t", t=PACK),
-            in_=wu_raw[:].rearrange("p a i (m t) -> p a m i t", t=PACK),
-        )
-        quantize_x(1, 2)
-        for a in range(PASSES):
-            quantize(wu_c[a][:], wu_s[a][:], xbh[a][0].rearrange("p j t -> p (j t)"))
-        quantize_x(1, 3)
-
-        wd_b = xbh[0][1].rearrange("p (t m) i -> p t m i", t=PACK)
         wd_c = tile("wd_c", [P, N], U32)
         wd_s = tile("wd_s", [P, N], U8)
 
         tg = [tile("tg%d" % h, [P, PACK, HALF], F32) for h in range(2)]
-        hb = [tile("hb%d" % q, [P, QUART, PACK], BF16) for q in range(4)]
-        hc = [tile("hc%d" % q, [P, QUART], U32) for q in range(4)]
-        hs = [tile("hs%d" % q, [P, QUART], U8) for q in range(4)]
-        o_sb = [[tile("o%d%d" % (q, u), [P, 2, QUART], F32) for u in range(2)] for q in range(4)]
+        hb = [tile("hb%d" % q, [P, w, PACK], BF16) for q, (j0, w) in enumerate(GROUPS)]
+        hc = [tile("hc%d" % q, [P, w], U32) for q, (j0, w) in enumerate(GROUPS)]
+        hs = [tile("hs%d" % q, [P, w], U8) for q, (j0, w) in enumerate(GROUPS)]
+        o_sb = [[tile("o%d%d" % (q, u), [P, 2, w], F32) for u in range(2)] for q, (j0, w) in enumerate(GROUPS)]
         out_v = out.rearrange("(p c) j -> p c j", c=PACK)
 
-        ga = [[ps.tile([P, HALF], F32, name="ga%d%d" % (h, t), tag="bank") for t in range(PACK)] for h in range(2)]
+        ga = [[ps[h].tile([P, HALF], F32, name="ga%d%d" % (h, t), tag="bank") for t in range(PACK)] for h in range(2)]
 
         def gate(h, a):
             cols = slice(h * HALF, (h + 1) * HALF)
@@ -164,15 +181,16 @@ def tile_list_tanh_bias_kernel(tc, xT, wgt, wg_words, wg_scales, wu, wd, b, offs
                     stop=(a == PASSES - 1),
                 )
 
-        def gate_tanh(h):
+        def gate_tanh(h, c0, w):
             for t in range(PACK):
-                nc.scalar.activation(out=tg[h][:, t, :], in_=ga[h][t][:], func=ACT.Tanh)
+                nc.scalar.activation(out=tg[h][:, t, c0 : c0 + w], in_=ga[h][t][:, c0 : c0 + w], func=ACT.Tanh)
 
         def up(c):
-            q, c0 = divmod(c * CH, QUART)
+            q = max(k for k, (j0, w) in enumerate(GROUPS) if j0 <= c * CH)
+            c0 = c * CH - GROUPS[q][0]
             h, h0 = divmod(c * CH, HALF)
             cols = slice(c * CH, (c + 1) * CH)
-            acc = ps.tile([P, PACK, CH], F32, name="ub", tag="bank")
+            acc = ps[0].tile([P, PACK, CH], F32, name="ub", tag="bank")
             for t in range(PACK):
                 for a in range(PASSES):
                     nc.tensor.matmul_mx(
@@ -184,7 +202,7 @@ def tile_list_tanh_bias_kernel(tc, xT, wgt, wg_words, wg_scales, wu, wd, b, offs
                         start=(a == 0),
                         stop=(a == PASSES - 1),
                     )
-            nc.vector.tensor_tensor(
+            return lambda: nc.vector.tensor_tensor(
                 hb[q][:, c0 : c0 + CH, :].rearrange("p (c i) t -> p c t i", i=4),
                 acc[:].rearrange("p t (c i) -> p c t i", i=4),
                 tg[h][:, :, h0 : h0 + CH].rearrange("p t (c i) -> p c t i", i=4),
@@ -192,8 +210,9 @@ def tile_list_tanh_bias_kernel(tc, xT, wgt, wg_words, wg_scales, wu, wd, b, offs
             )
 
         def down(q):
+            j0, w = GROUPS[q]
             for u in range(2):
-                acc = ps.tile([P, 2, QUART], F32, name="y", tag="bank")
+                acc = ps[1 if w == QUART else 0].tile([P, 2, w], F32, name="y", tag="bank")
                 for v in range(2):
                     c = 2 * u + v
                     nc.tensor.matmul_mx(
@@ -207,27 +226,42 @@ def tile_list_tanh_bias_kernel(tc, xT, wgt, wg_words, wg_scales, wu, wd, b, offs
                     )
                 for v in range(2):
                     c = 2 * u + v
-                    if q == 3 and u == 1:
+                    if q in (2, 4) and u == 1:
                         nc.vector.tensor_scalar_add(o_sb[q][u][:, v, :], acc[:, v, :], bias[:, c : c + 1])
                     else:
                         nc.scalar.activation(out=o_sb[q][u][:, v, :], in_=acc[:, v, :], func=ACT.Identity, bias=bias[:, c : c + 1])
-                nc.sync.dma_start(out=out_v[:, 2 * u : 2 * u + 2, q * QUART : (q + 1) * QUART], in_=o_sb[q][u][:])
+                nc.sync.dma_start(out=out_v[:, 2 * u : 2 * u + 2, j0 : j0 + w], in_=o_sb[q][u][:])
 
-        for a in range(PASSES):
-            for h in range(2):
-                gate(h, a)
-        gate_tanh(0)
-        o, s = weight_views(wd_raw, wd_b)
-        nc.scalar.copy(out=o[:, 0:64], in_=s[:, 0:64])
-        gate_tanh(1)
-        for q in range(4):
-            up(2 * q)
-            up(2 * q + 1)
-            if q == 0:
-                nc.vector.tensor_copy(out=o[:, 64:128], in_=s[:, 64:128])
+        def quantize_h(q):
             quantize(hc[q][:], hs[q][:], hb[q][:].rearrange("p j t -> p (j t)"))
-            if q == 0:
-                quantize(wd_c[:], wd_s[:], wd_b.rearrange("p t m i -> p (t m i)"))
-            else:
-                down(q - 1)
-        down(3)
+
+        gate(0, 0)
+        gate(1, 0)
+        gate(0, 1)
+        gate_tanh(0, 0, HALF)
+        interleave_w(nc.scalar.copy, wd_raw[:], wd_b)
+        products = [up(c) for c in range(3)]
+        gate(1, 1)
+        gate_tanh(1, 0, HALF)
+        products.append(up(3))
+        products[0]()
+        products.append(up(4))
+        products[1]()
+        products.append(up(5))
+        products[2]()
+        quantize_h(0)
+        quantize(wd_c[:], wd_s[:], wd_b.rearrange("p t m i -> p (t m i)"))
+        down(0)
+        products.append(up(6))
+        products[3]()
+        quantize_h(1)
+        down(1)
+        products.append(up(7))
+        for c in range(4, 7):
+            products[c]()
+        quantize_h(2)
+        quantize_h(3)
+        products[7]()
+        quantize_h(4)
+        for q in range(2, 5):
+            down(q)

@@ -18,250 +18,272 @@ MULT = mybir.AluOpType.mult
 
 P = 128
 PACK = 4
-KP = P * PACK
-PASSES = K // KP
-HALF = 512
-QUART = 256
-CH = 128
+PASS_K = P * PACK
+PASSES = K // PASS_K
+LIST_ROWS = 16
+QUADRANT = 32
+RUN = 4
+HALF = J // 2
+QUARTER = J // 4
+CHUNK = 128
 GROUPS = [(0, 256), (256, 256), (512, 256), (768, 128), (896, 128)]
+VECTOR_EMPTIES = (2, 4)
+WU_SPLIT = P // 2
 
 
 def tile_list_tanh_bias_kernel(tc, xT, wgt, wg_words, wg_scales, wu, wd, b, offs, out):
     nc = tc.nc
     with ExitStack() as ctx:
         sb = ctx.enter_context(tc.tile_pool(name="sb", bufs=1))
-        ps = [ctx.enter_context(tc.psum_pool(name="ps%d" % h, bufs=PACK)) for h in range(2)]
+        psum = [ctx.enter_context(tc.psum_pool(name="psum%d" % h, bufs=PACK)) for h in range(2)]
 
         def tile(name, shape, dtype):
             return sb.tile(shape, dtype, name=name, align_bytes=64)
 
-        offsets = sb.tile([P, J // 16], U16, name="offsets")
-        wg_raw = tile("wg_raw", [P, PASSES, 2 * R], U8)
-        sg_raw = tile("sg_raw", [P, PASSES, R], U8)
-        wg_c = tile("wg_c", [P, PASSES, PACK, 2 * P], U8)
-        wg_s = tile("wg_s", [P, PASSES, PACK, P], U8)
-        g1 = tile("g1", [P, PACK + 2, HALF], F32)
-        wgt_sb = [g1[:, 1, :], tile("wgt1", [P, HALF], F32)[:]]
-        x_sb = [[tile("x%d%d" % (a, i), [P, T], F32) for i in range(PACK)] for a in range(PASSES)]
+        offsets = sb.tile([P, J // LIST_ROWS], U16, name="offsets")
+        wg_words_raw = tile("wg_words_raw", [P, PASSES, 2 * R], U8)
+        wg_scales_raw = tile("wg_scales_raw", [P, PASSES, R], U8)
+        wg_codes = tile("wg_codes", [P, PASSES, PACK, 2 * P], U8)
+        wg_scale = tile("wg_scale", [P, PASSES, PACK, P], U8)
+
+        shared = tile("shared", [P, PACK + 2, HALF], F32)
+        wgt_half = [shared[:, 1, :], tile("wgt_second", [P, HALF], F32)[:]]
+        planes = [[tile("plane%d%d" % (a, i), [P, T], F32) for i in range(PACK)] for a in range(PASSES)]
         wu_raw = tile("wu_raw", [P, PASSES, PACK, R], F32)
         wd_raw = tile("wd_raw", [P, PACK, N], F32)
         bias = tile("bias", [P, PACK], F32)
-        warm = tile("warm", [P, 16], F32)
 
-        nc.vector.memset(sg_raw[:].rearrange("p a r -> p (a r)").bitcast(I32), 0)
-        nc.vector.memset(warm[:, 0:8], 0.0)
+        nc.vector.memset(wg_scales_raw[:].rearrange("p a r -> p (a r)").bitcast(I32), 0)
         nc.sync.dma_start(offsets[:], offs)
-        nc.sync.dma_start(out=wg_raw[:].bitcast(I32), in_=wg_words.rearrange("a p n -> p a n").bitcast(I32))
-        nc.sync.dma_start(out=wgt_sb[0], in_=wgt[:, 0:HALF])
-        for q in range(4):
+        nc.sync.dma_start(out=wg_words_raw[:].bitcast(I32), in_=wg_words.rearrange("a p n -> p a n").bitcast(I32))
+        nc.sync.dma_start(out=wgt_half[0], in_=wgt[:, 0:HALF])
+        for q in range(P // QUADRANT):
             nc.sync.dma_start(
-                out=sg_raw[32 * q : 32 * q + 4, :, :].bitcast(I32),
+                out=wg_scales_raw[QUADRANT * q : QUADRANT * q + 4, :, :].bitcast(I32),
                 in_=wg_scales[:, 4 * q : 4 * q + 4, :].rearrange("a r n -> r a n").bitcast(I32),
             )
-        nc.scalar.activation(out=warm[:, 8:16], in_=warm[:, 0:8], func=ACT.Tanh)
-
-        def load_x(plane):
-            a, i = divmod(plane, PACK)
-            rows = xT[a * KP : (a + 1) * KP, :].rearrange("(p i) t -> p i t", i=PACK)
-            nc.sync.dma_start(out=x_sb[a][i][:], in_=rows[:, i, :])
-
-        def load_wu(a):
-            nc.sync.dma_start(out=wu_raw[:, a, :, :], in_=wu[a * KP : (a + 1) * KP, :].rearrange("(p i) r -> p i r", i=PACK))
-
-        load_x(0)
-        nc.sync.dma_start(out=wgt_sb[1], in_=wgt[:, HALF:J])
-        for plane in range(1, 8):
-            load_x(plane)
-        load_wu(0)
-        load_wu(1)
+        for a in range(PASSES):
+            rows = xT[a * PASS_K : (a + 1) * PASS_K, :].rearrange("(p i) t -> p i t", i=PACK)
+            for i in range(PACK):
+                nc.sync.dma_start(out=planes[a][i][:], in_=rows[:, i, :])
+                if (a, i) == (0, 0):
+                    nc.sync.dma_start(out=wgt_half[1], in_=wgt[:, HALF:J])
+        for a in range(PASSES):
+            rows = wu[a * PASS_K : (a + 1) * PASS_K, :].rearrange("(p i) r -> p i r", i=PACK)
+            nc.sync.dma_start(out=wu_raw[:, a, :, :], in_=rows)
         nc.sync.dma_start(out=wd_raw[:], in_=wd.rearrange("(p i) n -> p i n", i=PACK))
-        nc.sync.dma_start(out=bias[:], in_=b.rearrange("(p c) -> p c", c=PACK))
+        nc.sync.dma_start(out=bias[:], in_=b.rearrange("(p t) -> p t", t=PACK))
 
         nc.vector.tensor_copy(
-            out=wg_c[:].bitcast(U16),
-            in_=wg_raw[:].bitcast(U16).rearrange("p a (m t) -> p a t m", t=PACK),
+            out=wg_codes[:].bitcast(U16),
+            in_=wg_words_raw[:].bitcast(U16).rearrange("p a (m t) -> p a t m", t=PACK),
         )
         nc.vector.tensor_copy(
-            out=wg_s[:],
-            in_=sg_raw[:].rearrange("p a (m t) -> p a t m", t=PACK),
+            out=wg_scale[:],
+            in_=wg_scales_raw[:].rearrange("p a (m t) -> p a t m", t=PACK),
         )
 
-        g = [[tile("g0%d" % h, [P, PACK, HALF], F32)[:] for h in range(2)], [g1[:, 2 : PACK + 2, :], g1[:, 0:PACK, :]]]
-        xbh = [[tile("xb%d%d" % (a, h), [P, HALF, PACK], BF16)[:] for h in range(2)] for a in range(PASSES)]
-        xc = [tile("xc%d" % a, [P, J], U32) for a in range(PASSES)]
-        xs = [tile("xs%d" % a, [P, J], U8) for a in range(PASSES)]
+        xg = [
+            [tile("xg0%d" % h, [P, PACK, HALF], F32)[:] for h in range(2)],
+            [shared[:, 2 : PACK + 2, :], shared[:, 0:PACK, :]],
+        ]
+        xg_bf16 = [[tile("xg_bf16_%d%d" % (a, h), [P, HALF, PACK], BF16)[:] for h in range(2)] for a in range(PASSES)]
+        xg_codes = [tile("xg_codes%d" % a, [P, J], U32) for a in range(PASSES)]
+        xg_scale = [tile("xg_scale%d" % a, [P, J], U8) for a in range(PASSES)]
 
-        def gather(a, i, j0, w):
+        def gather(a, i, j0, width):
             h, c0 = divmod(j0, HALF)
             nc.vector.tensor_tensor(
-                g[a][h][:, i, c0 : c0 + w],
-                x_sb[a][i][:].indirect(offsets[:, j0 // 16 : (j0 + w) // 16]),
-                wgt_sb[h][:, c0 : c0 + w],
+                xg[a][h][:, i, c0 : c0 + width],
+                planes[a][i][:].indirect(offsets[:, j0 // LIST_ROWS : (j0 + width) // LIST_ROWS]),
+                wgt_half[h][:, c0 : c0 + width],
                 MULT,
             )
 
-        def interleave_x(copy, a, j0, w):
+        def activation_copy(out, in_):
+            nc.scalar.activation(out=out, in_=in_, func=ACT.Copy)
+
+        def interleave_xg(copy, a, j0, width):
             h, c0 = divmod(j0, HALF)
             copy(
-                out=xbh[a][h][:, c0 : c0 + w, :].rearrange("p (c i) t -> p c t i", i=4),
-                in_=g[a][h][:, :, c0 : c0 + w].rearrange("p t (c i) -> p c t i", i=4),
+                out=xg_bf16[a][h][:, c0 : c0 + width, :].rearrange("p (c e) i -> p c i e", e=RUN),
+                in_=xg[a][h][:, :, c0 : c0 + width].rearrange("p i (c e) -> p c i e", e=RUN),
             )
 
-        def quantize(codes, scales, src):
-            nc.vector.quantize_mx(out=codes.bitcast(FP8X4), scales=scales, in_=src)
+        def quantize(codes, scale, src):
+            nc.vector.quantize_mx(out=codes.bitcast(FP8X4), scales=scale, in_=src)
 
-        def quantize_x(a, j0, w):
+        def quantize_xg(a, j0, width):
             h, c0 = divmod(j0, HALF)
-            cols = slice(j0, j0 + w)
-            quantize(xc[a][:, cols], xs[a][:, cols], xbh[a][h][:, c0 : c0 + w, :].rearrange("p j t -> p (j t)"))
+            cols = slice(j0, j0 + width)
+            src = xg_bf16[a][h][:, c0 : c0 + width, :].rearrange("p j i -> p (j i)")
+            quantize(xg_codes[a][:, cols], xg_scale[a][:, cols], src)
 
-        def interleave_w(copy, raw, dst, m0=0, m1=P):
-            copy(out=dst.rearrange("p t m i -> p m i t")[:, m0:m1], in_=raw.rearrange("p i (m t) -> p m i t", t=PACK)[:, m0:m1])
+        def interleave_weight(copy, raw, dst, m0, m1):
+            copy(
+                out=dst.rearrange("p t m i -> p m i t")[:, m0:m1],
+                in_=raw.rearrange("p i (m t) -> p m i t", t=PACK)[:, m0:m1],
+            )
 
-        g1_tail = g1[:].rearrange("p s j -> p (s j)")[:, 3 * HALF + QUART : 5 * HALF + QUART].bitcast(BF16)
-        wu_b = [tile("wu_b0", [P, PACK, P, PACK], BF16)[:], g1_tail.rearrange("p (t m i) -> p t m i", t=PACK, i=PACK)]
-        wu_c = [tile("wu_c%d" % a, [P, R], U32) for a in range(PASSES)]
-        wu_s = [tile("wu_s%d" % a, [P, R], U8) for a in range(PASSES)]
-        wd_b = tile("wd_b", [P, PACK, P, PACK], BF16)[:]
+        wu_staging = shared[:].rearrange("p s j -> p (s j)")[:, 3 * HALF + QUARTER : 5 * HALF + QUARTER].bitcast(BF16)
+        wu_bf16 = [
+            tile("wu_bf16_0", [P, PACK, P, PACK], BF16)[:],
+            wu_staging.rearrange("p (t m i) -> p t m i", t=PACK, i=PACK),
+        ]
+        wu_codes = [tile("wu_codes%d" % a, [P, R], U32) for a in range(PASSES)]
+        wu_scale = [tile("wu_scale%d" % a, [P, R], U8) for a in range(PASSES)]
+        wd_bf16 = tile("wd_bf16", [P, PACK, P, PACK], BF16)[:]
 
         def quantize_wu(a):
-            quantize(wu_c[a][:], wu_s[a][:], wu_b[a].rearrange("p t m i -> p (t m i)"))
+            quantize(wu_codes[a][:], wu_scale[a][:], wu_bf16[a].rearrange("p t m i -> p (t m i)"))
 
         for i in range(PACK):
             for h in range(2):
                 gather(0, i, h * HALF, HALF)
         for h in range(2):
-            interleave_x(nc.scalar.copy, 0, h * HALF, HALF)
+            interleave_xg(activation_copy, 0, h * HALF, HALF)
+
         gather(1, 0, 0, HALF)
         gather(1, 0, HALF, HALF)
         gather(1, 1, 0, HALF)
-        quantize_x(0, 0, HALF)
+        quantize_xg(0, 0, HALF)
         gather(1, 2, 0, HALF)
-        quantize_x(0, HALF, HALF)
-        for q in range(2):
-            gather(1, 3, q * QUART, QUART)
-            interleave_x(nc.scalar.copy, 1, q * QUART, QUART)
-        interleave_w(nc.scalar.copy, wu_raw[:, 0, :, :], wu_b[0])
-        interleave_w(nc.scalar.copy, wu_raw[:, 1, :, :], wu_b[1], 0, P // 2)
+        quantize_xg(0, HALF, HALF)
+        for quarter in range(2):
+            gather(1, 3, quarter * QUARTER, QUARTER)
+            interleave_xg(nc.scalar.copy, 1, quarter * QUARTER, QUARTER)
+
+        interleave_weight(nc.scalar.copy, wu_raw[:, 0, :, :], wu_bf16[0], 0, P)
+        interleave_weight(nc.scalar.copy, wu_raw[:, 1, :, :], wu_bf16[1], 0, WU_SPLIT)
         gather(1, 1, HALF, HALF)
-        quantize_x(1, 0, HALF)
+        quantize_xg(1, 0, HALF)
         gather(1, 2, HALF, HALF)
-        interleave_w(nc.vector.tensor_copy, wu_raw[:, 1, :, :], wu_b[1], P // 2, P)
+        interleave_weight(nc.vector.tensor_copy, wu_raw[:, 1, :, :], wu_bf16[1], WU_SPLIT, P)
         quantize_wu(0)
-        gather(1, 3, 2 * QUART, QUART)
+        gather(1, 3, 2 * QUARTER, QUARTER)
         quantize_wu(1)
-        gather(1, 3, 3 * QUART, QUART)
-        for q in range(2, 4):
-            interleave_x(nc.vector.tensor_copy, 1, q * QUART, QUART)
-        for q in range(2, 4):
-            quantize_x(1, q * QUART, QUART)
+        gather(1, 3, 3 * QUARTER, QUARTER)
+        for quarter in range(2, 4):
+            interleave_xg(nc.vector.tensor_copy, 1, quarter * QUARTER, QUARTER)
+        for quarter in range(2, 4):
+            quantize_xg(1, quarter * QUARTER, QUARTER)
 
-        wd_c = tile("wd_c", [P, N], U32)
-        wd_s = tile("wd_s", [P, N], U8)
+        wd_codes = tile("wd_codes", [P, N], U32)
+        wd_scale = tile("wd_scale", [P, N], U8)
+        tanh_ga = [tile("tanh_ga%d" % h, [P, PACK, HALF], F32) for h in range(2)]
+        h_bf16 = [tile("h_bf16_%d" % g, [P, width, PACK], BF16) for g, (j0, width) in enumerate(GROUPS)]
+        h_codes = [tile("h_codes%d" % g, [P, width], U32) for g, (j0, width) in enumerate(GROUPS)]
+        h_scale = [tile("h_scale%d" % g, [P, width], U8) for g, (j0, width) in enumerate(GROUPS)]
+        result = [
+            [tile("result%d%d" % (g, pair), [P, 2, width], F32) for pair in range(2)]
+            for g, (j0, width) in enumerate(GROUPS)
+        ]
+        out_rows = out.rearrange("(p t) j -> p t j", t=PACK)
 
-        tg = [tile("tg%d" % h, [P, PACK, HALF], F32) for h in range(2)]
-        hb = [tile("hb%d" % q, [P, w, PACK], BF16) for q, (j0, w) in enumerate(GROUPS)]
-        hc = [tile("hc%d" % q, [P, w], U32) for q, (j0, w) in enumerate(GROUPS)]
-        hs = [tile("hs%d" % q, [P, w], U8) for q, (j0, w) in enumerate(GROUPS)]
-        o_sb = [[tile("o%d%d" % (q, u), [P, 2, w], F32) for u in range(2)] for q, (j0, w) in enumerate(GROUPS)]
-        out_v = out.rearrange("(p c) j -> p c j", c=PACK)
+        ga = [
+            [psum[h].tile([P, HALF], F32, name="ga%d%d" % (h, t), tag="bank") for t in range(PACK)]
+            for h in range(2)
+        ]
 
-        ga = [[ps[h].tile([P, HALF], F32, name="ga%d%d" % (h, t), tag="bank") for t in range(PACK)] for h in range(2)]
-
-        def gate(h, a):
+        def gate_pass(h, a):
             cols = slice(h * HALF, (h + 1) * HALF)
             for t in range(PACK):
                 nc.tensor.matmul_mx(
                     out=ga[h][t][:],
-                    lhsT=wg_c[:, a, t, :].bitcast(FP4X4),
-                    lhsT_scale=wg_s[:, a, t, :],
-                    rhs=xc[a][:, cols].bitcast(FP8X4),
-                    rhs_scale=xs[a][:, cols],
+                    lhsT=wg_codes[:, a, t, :].bitcast(FP4X4),
+                    lhsT_scale=wg_scale[:, a, t, :],
+                    rhs=xg_codes[a][:, cols].bitcast(FP8X4),
+                    rhs_scale=xg_scale[a][:, cols],
                     start=(a == 0),
                     stop=(a == PASSES - 1),
                 )
 
-        def gate_tanh(h, c0, w):
+        def gate_tanh(h):
             for t in range(PACK):
-                nc.scalar.activation(out=tg[h][:, t, c0 : c0 + w], in_=ga[h][t][:, c0 : c0 + w], func=ACT.Tanh)
+                nc.scalar.activation(out=tanh_ga[h][:, t, :], in_=ga[h][t][:], func=ACT.Tanh)
 
-        def up(c):
-            q = max(k for k, (j0, w) in enumerate(GROUPS) if j0 <= c * CH)
-            c0 = c * CH - GROUPS[q][0]
-            h, h0 = divmod(c * CH, HALF)
-            cols = slice(c * CH, (c + 1) * CH)
-            acc = ps[0].tile([P, PACK, CH], F32, name="ub", tag="bank")
+        def up_product(chunk):
+            cols = slice(chunk * CHUNK, (chunk + 1) * CHUNK)
+            ub = psum[0].tile([P, PACK, CHUNK], F32, name="ub", tag="bank")
             for t in range(PACK):
                 for a in range(PASSES):
                     nc.tensor.matmul_mx(
-                        out=acc[:, t, :],
-                        lhsT=wu_c[a][:, t * P : (t + 1) * P].bitcast(FP8X4),
-                        lhsT_scale=wu_s[a][:, t * P : (t + 1) * P],
-                        rhs=xc[a][:, cols].bitcast(FP8X4),
-                        rhs_scale=xs[a][:, cols],
+                        out=ub[:, t, :],
+                        lhsT=wu_codes[a][:, t * P : (t + 1) * P].bitcast(FP8X4),
+                        lhsT_scale=wu_scale[a][:, t * P : (t + 1) * P],
+                        rhs=xg_codes[a][:, cols].bitcast(FP8X4),
+                        rhs_scale=xg_scale[a][:, cols],
                         start=(a == 0),
                         stop=(a == PASSES - 1),
                     )
-            return lambda: nc.vector.tensor_tensor(
-                hb[q][:, c0 : c0 + CH, :].rearrange("p (c i) t -> p c t i", i=4),
-                acc[:].rearrange("p t (c i) -> p c t i", i=4),
-                tg[h][:, :, h0 : h0 + CH].rearrange("p t (c i) -> p c t i", i=4),
+            return ub
+
+        def form_h(chunk, ub):
+            g = max(k for k, (j0, width) in enumerate(GROUPS) if j0 <= chunk * CHUNK)
+            in_group = chunk * CHUNK - GROUPS[g][0]
+            h, in_half = divmod(chunk * CHUNK, HALF)
+            nc.vector.tensor_tensor(
+                h_bf16[g][:, in_group : in_group + CHUNK, :].rearrange("p (c e) t -> p c t e", e=RUN),
+                ub[:].rearrange("p t (c e) -> p c t e", e=RUN),
+                tanh_ga[h][:, :, in_half : in_half + CHUNK].rearrange("p t (c e) -> p c t e", e=RUN),
                 MULT,
             )
 
-        def down(q):
-            j0, w = GROUPS[q]
-            for u in range(2):
-                acc = ps[1 if w == QUART else 0].tile([P, 2, w], F32, name="y", tag="bank")
+        def quantize_h(g):
+            quantize(h_codes[g][:], h_scale[g][:], h_bf16[g][:].rearrange("p j t -> p (j t)"))
+
+        def down_product(g):
+            j0, width = GROUPS[g]
+            for pair in range(2):
+                y = psum[1 if width == QUARTER else 0].tile([P, 2, width], F32, name="y", tag="bank")
                 for v in range(2):
-                    c = 2 * u + v
+                    t = 2 * pair + v
                     nc.tensor.matmul_mx(
-                        out=acc[:, v, :],
-                        lhsT=wd_c[:, c * P : (c + 1) * P].bitcast(FP8X4),
-                        lhsT_scale=wd_s[:, c * P : (c + 1) * P],
-                        rhs=hc[q][:].bitcast(FP8X4),
-                        rhs_scale=hs[q][:],
+                        out=y[:, v, :],
+                        lhsT=wd_codes[:, t * P : (t + 1) * P].bitcast(FP8X4),
+                        lhsT_scale=wd_scale[:, t * P : (t + 1) * P],
+                        rhs=h_codes[g][:].bitcast(FP8X4),
+                        rhs_scale=h_scale[g][:],
                         start=True,
                         stop=True,
                     )
                 for v in range(2):
-                    c = 2 * u + v
-                    if q in (2, 4) and u == 1:
-                        nc.vector.tensor_scalar_add(o_sb[q][u][:, v, :], acc[:, v, :], bias[:, c : c + 1])
+                    t = 2 * pair + v
+                    dst = result[g][pair][:, v, :]
+                    if g in VECTOR_EMPTIES and pair == 1:
+                        nc.vector.tensor_scalar_add(dst, y[:, v, :], bias[:, t : t + 1])
                     else:
-                        nc.scalar.activation(out=o_sb[q][u][:, v, :], in_=acc[:, v, :], func=ACT.Identity, bias=bias[:, c : c + 1])
-                nc.sync.dma_start(out=out_v[:, 2 * u : 2 * u + 2, j0 : j0 + w], in_=o_sb[q][u][:])
+                        nc.scalar.activation(out=dst, in_=y[:, v, :], func=ACT.Identity, bias=bias[:, t : t + 1])
+                nc.sync.dma_start(out=out_rows[:, 2 * pair : 2 * pair + 2, j0 : j0 + width], in_=result[g][pair][:])
 
-        def quantize_h(q):
-            quantize(hc[q][:], hs[q][:], hb[q][:].rearrange("p j t -> p (j t)"))
+        gate_pass(0, 0)
+        gate_pass(1, 0)
+        gate_pass(0, 1)
+        gate_tanh(0)
+        interleave_weight(nc.scalar.copy, wd_raw[:], wd_bf16, 0, P)
 
-        gate(0, 0)
-        gate(1, 0)
-        gate(0, 1)
-        gate_tanh(0, 0, HALF)
-        interleave_w(nc.scalar.copy, wd_raw[:], wd_b)
-        products = [up(c) for c in range(3)]
-        gate(1, 1)
-        gate_tanh(1, 0, HALF)
-        products.append(up(3))
-        products[0]()
-        products.append(up(4))
-        products[1]()
-        products.append(up(5))
-        products[2]()
+        ub = [up_product(chunk) for chunk in range(3)]
+        gate_pass(1, 1)
+        gate_tanh(1)
+        ub.append(up_product(3))
+        form_h(0, ub[0])
+        ub.append(up_product(4))
+        form_h(1, ub[1])
+        ub.append(up_product(5))
+        form_h(2, ub[2])
         quantize_h(0)
-        quantize(wd_c[:], wd_s[:], wd_b.rearrange("p t m i -> p (t m i)"))
-        down(0)
-        products.append(up(6))
-        products[3]()
+        quantize(wd_codes[:], wd_scale[:], wd_bf16.rearrange("p t m i -> p (t m i)"))
+        down_product(0)
+        ub.append(up_product(6))
+        form_h(3, ub[3])
         quantize_h(1)
-        down(1)
-        products.append(up(7))
-        for c in range(4, 7):
-            products[c]()
+        down_product(1)
+        ub.append(up_product(7))
+        for chunk in range(4, 7):
+            form_h(chunk, ub[chunk])
         quantize_h(2)
         quantize_h(3)
-        products[7]()
+        form_h(7, ub[7])
         quantize_h(4)
-        for q in range(2, 5):
-            down(q)
+        for g in range(2, len(GROUPS)):
+            down_product(g)

@@ -25,10 +25,12 @@ QUADRANT = 32
 RUN = 4
 HALF = J // 2
 QUARTER = J // 4
+SLOT = QUARTER + J
 CHUNK = 128
 GROUPS = [(0, 256), (256, 256), (512, 256), (768, 128), (896, 128)]
-VECTOR_EMPTIES = (2, 4)
+VECTOR_EMPTIES = (2, 3, 4)
 WU_SPLIT = P // 2
+WD_SPLIT = 3 * P // 4
 
 
 def tile_list_tanh_bias_kernel(tc, xT, wgt, wg_words, wg_scales, wu, wd, b, offs, out):
@@ -37,8 +39,8 @@ def tile_list_tanh_bias_kernel(tc, xT, wgt, wg_words, wg_scales, wu, wd, b, offs
         sb = ctx.enter_context(tc.tile_pool(name="sb", bufs=1))
         psum = [ctx.enter_context(tc.psum_pool(name="psum%d" % h, bufs=PACK)) for h in range(2)]
 
-        def tile(name, shape, dtype):
-            return sb.tile(shape, dtype, name=name, align_bytes=64)
+        def tile(name, shape, dtype, tag=None):
+            return sb.tile(shape, dtype, name=name, tag=tag or name, align_bytes=64)
 
         offsets = sb.tile([P, J // LIST_ROWS], U16, name="offsets")
         wg_words_raw = tile("wg_words_raw", [P, PASSES, 2 * R], U8)
@@ -46,17 +48,17 @@ def tile_list_tanh_bias_kernel(tc, xT, wgt, wg_words, wg_scales, wu, wd, b, offs
         wg_codes = tile("wg_codes", [P, PASSES, PACK, 2 * P], U8)
         wg_scale = tile("wg_scale", [P, PASSES, PACK, P], U8)
 
-        shared = tile("shared", [P, PACK + 2, HALF], F32)
-        wgt_half = [shared[:, 1, :], tile("wgt_second", [P, HALF], F32)[:]]
+        shared = tile("shared", [P, PACK + 2, SLOT], F32)
+        wgt_sb = shared[:, 1, QUARTER:SLOT]
         planes = [[tile("plane%d%d" % (a, i), [P, T], F32) for i in range(PACK)] for a in range(PASSES)]
-        wu_raw = tile("wu_raw", [P, PASSES, PACK, R], F32)
+        wu_raw = [tile("wu_raw%d" % a, [P, PACK, R], F32) for a in range(PASSES)]
         wd_raw = tile("wd_raw", [P, PACK, N], F32)
         bias = tile("bias", [P, PACK], F32)
 
         nc.vector.memset(wg_scales_raw[:].rearrange("p a r -> p (a r)").bitcast(I32), 0)
         nc.sync.dma_start(offsets[:], offs)
         nc.sync.dma_start(out=wg_words_raw[:].bitcast(I32), in_=wg_words.rearrange("a p n -> p a n").bitcast(I32))
-        nc.sync.dma_start(out=wgt_half[0], in_=wgt[:, 0:HALF])
+        nc.sync.dma_start(out=wgt_sb[:, 0:HALF], in_=wgt[:, 0:HALF])
         for q in range(P // QUADRANT):
             nc.sync.dma_start(
                 out=wg_scales_raw[QUADRANT * q : QUADRANT * q + 4, :, :].bitcast(I32),
@@ -67,10 +69,10 @@ def tile_list_tanh_bias_kernel(tc, xT, wgt, wg_words, wg_scales, wu, wd, b, offs
             for i in range(PACK):
                 nc.sync.dma_start(out=planes[a][i][:], in_=rows[:, i, :])
                 if (a, i) == (0, 0):
-                    nc.sync.dma_start(out=wgt_half[1], in_=wgt[:, HALF:J])
+                    nc.sync.dma_start(out=wgt_sb[:, HALF:J], in_=wgt[:, HALF:J])
         for a in range(PASSES):
             rows = wu[a * PASS_K : (a + 1) * PASS_K, :].rearrange("(p i) r -> p i r", i=PACK)
-            nc.sync.dma_start(out=wu_raw[:, a, :, :], in_=rows)
+            nc.sync.dma_start(out=wu_raw[a][:], in_=rows)
         nc.sync.dma_start(out=wd_raw[:], in_=wd.rearrange("(p i) n -> p i n", i=PACK))
         nc.sync.dma_start(out=bias[:], in_=b.rearrange("(p t) -> p t", t=PACK))
 
@@ -83,20 +85,26 @@ def tile_list_tanh_bias_kernel(tc, xT, wgt, wg_words, wg_scales, wu, wd, b, offs
             in_=wg_scales_raw[:].rearrange("p a (m t) -> p a t m", t=PACK),
         )
 
+        xg_first = tile("xg_first", [P, PACK, J], F32)
         xg = [
-            [tile("xg0%d" % h, [P, PACK, HALF], F32)[:] for h in range(2)],
-            [shared[:, 2 : PACK + 2, :], shared[:, 0:PACK, :]],
+            [xg_first[:, :, h * HALF : (h + 1) * HALF] for h in range(2)],
+            [shared[:, 2 : PACK + 2, 0:HALF], shared[:, 0:PACK, 0:HALF]],
         ]
-        xg_bf16 = [[tile("xg_bf16_%d%d" % (a, h), [P, HALF, PACK], BF16)[:] for h in range(2)] for a in range(PASSES)]
+        wu_bf16 = [tile("wu_bf16_%d" % a, [P, PACK, P, PACK], BF16)[:] for a in range(PASSES)]
+        after_wu = tile("after_wu", [P, (PACK + 2) * HALF], F32, tag="wu_raw1")
+        xg_bf16 = [
+            [tile("xg_bf16_0%d" % h, [P, HALF, PACK], BF16)[:] for h in range(2)],
+            [tile("xg_bf16_10", [P, HALF, PACK], BF16)[:], after_wu[:, PACK * HALF :].bitcast(BF16).rearrange("p (j i) -> p j i", i=PACK)],
+        ]
         xg_codes = [tile("xg_codes%d" % a, [P, J], U32) for a in range(PASSES)]
         xg_scale = [tile("xg_scale%d" % a, [P, J], U8) for a in range(PASSES)]
 
         def gather(a, i, j0, width):
             h, c0 = divmod(j0, HALF)
             nc.vector.tensor_tensor(
-                xg[a][h][:, i, c0 : c0 + width],
+                xg_first[:, i, :] if width == J else xg[a][h][:, i, c0 : c0 + width],
                 planes[a][i][:].indirect(offsets[:, j0 // LIST_ROWS : (j0 + width) // LIST_ROWS]),
-                wgt_half[h][:, c0 : c0 + width],
+                wgt_sb[:, j0 : j0 + width],
                 MULT,
             )
 
@@ -125,11 +133,6 @@ def tile_list_tanh_bias_kernel(tc, xT, wgt, wg_words, wg_scales, wu, wd, b, offs
                 in_=raw.rearrange("p i (m t) -> p m i t", t=PACK)[:, m0:m1],
             )
 
-        wu_staging = shared[:].rearrange("p s j -> p (s j)")[:, 3 * HALF + QUARTER : 5 * HALF + QUARTER].bitcast(BF16)
-        wu_bf16 = [
-            tile("wu_bf16_0", [P, PACK, P, PACK], BF16)[:],
-            wu_staging.rearrange("p (t m i) -> p t m i", t=PACK, i=PACK),
-        ]
         wu_codes = [tile("wu_codes%d" % a, [P, R], U32) for a in range(PASSES)]
         wu_scale = [tile("wu_scale%d" % a, [P, R], U8) for a in range(PASSES)]
         wd_bf16 = tile("wd_bf16", [P, PACK, P, PACK], BF16)[:]
@@ -138,8 +141,11 @@ def tile_list_tanh_bias_kernel(tc, xT, wgt, wg_words, wg_scales, wu, wd, b, offs
             quantize(wu_codes[a][:], wu_scale[a][:], wu_bf16[a].rearrange("p t m i -> p (t m i)"))
 
         for i in range(PACK):
-            for h in range(2):
-                gather(0, i, h * HALF, HALF)
+            if i in (0, PACK - 1):
+                gather(0, i, 0, HALF)
+                gather(0, i, HALF, HALF)
+            else:
+                gather(0, i, 0, J)
         for h in range(2):
             interleave_xg(activation_copy, 0, h * HALF, HALF)
 
@@ -153,16 +159,15 @@ def tile_list_tanh_bias_kernel(tc, xT, wgt, wg_words, wg_scales, wu, wd, b, offs
             gather(1, 3, quarter * QUARTER, QUARTER)
             interleave_xg(nc.scalar.copy, 1, quarter * QUARTER, QUARTER)
 
-        interleave_weight(nc.scalar.copy, wu_raw[:, 0, :, :], wu_bf16[0], 0, P)
-        interleave_weight(nc.scalar.copy, wu_raw[:, 1, :, :], wu_bf16[1], 0, WU_SPLIT)
+        interleave_weight(nc.scalar.copy, wu_raw[0][:], wu_bf16[0], 0, WU_SPLIT)
+        interleave_weight(nc.scalar.copy, wu_raw[1][:], wu_bf16[1], 0, P)
         gather(1, 1, HALF, HALF)
         quantize_xg(1, 0, HALF)
+        interleave_weight(nc.vector.tensor_copy, wu_raw[0][:], wu_bf16[0], WU_SPLIT, P)
         gather(1, 2, HALF, HALF)
-        interleave_weight(nc.vector.tensor_copy, wu_raw[:, 1, :, :], wu_bf16[1], WU_SPLIT, P)
+        gather(1, 3, HALF, HALF)
         quantize_wu(0)
-        gather(1, 3, 2 * QUARTER, QUARTER)
         quantize_wu(1)
-        gather(1, 3, 3 * QUARTER, QUARTER)
         for quarter in range(2, 4):
             interleave_xg(nc.vector.tensor_copy, 1, quarter * QUARTER, QUARTER)
         for quarter in range(2, 4):
@@ -170,7 +175,10 @@ def tile_list_tanh_bias_kernel(tc, xT, wgt, wg_words, wg_scales, wu, wd, b, offs
 
         wd_codes = tile("wd_codes", [P, N], U32)
         wd_scale = tile("wd_scale", [P, N], U8)
-        tanh_ga = [tile("tanh_ga%d" % h, [P, PACK, HALF], F32) for h in range(2)]
+        tanh_ga = [
+            after_wu[:, 0 : PACK * HALF].rearrange("p (t j) -> p t j", t=PACK),
+            tile("tanh_ga1", [P, PACK, HALF], F32)[:],
+        ]
         h_bf16 = [tile("h_bf16_%d" % g, [P, width, PACK], BF16) for g, (j0, width) in enumerate(GROUPS)]
         h_codes = [tile("h_codes%d" % g, [P, width], U32) for g, (j0, width) in enumerate(GROUPS)]
         h_scale = [tile("h_scale%d" % g, [P, width], U8) for g, (j0, width) in enumerate(GROUPS)]
@@ -260,7 +268,8 @@ def tile_list_tanh_bias_kernel(tc, xT, wgt, wg_words, wg_scales, wu, wd, b, offs
         gate_pass(1, 0)
         gate_pass(0, 1)
         gate_tanh(0)
-        interleave_weight(nc.scalar.copy, wd_raw[:], wd_bf16, 0, P)
+        interleave_weight(nc.scalar.copy, wd_raw[:], wd_bf16, 0, WD_SPLIT)
+        interleave_weight(nc.vector.tensor_copy, wd_raw[:], wd_bf16, WD_SPLIT, P)
 
         ub = [up_product(chunk) for chunk in range(3)]
         gate_pass(1, 1)
@@ -272,18 +281,18 @@ def tile_list_tanh_bias_kernel(tc, xT, wgt, wg_words, wg_scales, wu, wd, b, offs
         ub.append(up_product(5))
         form_h(2, ub[2])
         quantize_h(0)
-        quantize(wd_codes[:], wd_scale[:], wd_bf16.rearrange("p t m i -> p (t m i)"))
-        down_product(0)
         ub.append(up_product(6))
         form_h(3, ub[3])
+        quantize(wd_codes[:], wd_scale[:], wd_bf16.rearrange("p t m i -> p (t m i)"))
         quantize_h(1)
+        down_product(0)
         down_product(1)
         ub.append(up_product(7))
         for chunk in range(4, 7):
             form_h(chunk, ub[chunk])
         quantize_h(2)
-        quantize_h(3)
         form_h(7, ub[7])
+        quantize_h(3)
         quantize_h(4)
         for g in range(2, len(GROUPS)):
             down_product(g)

@@ -15,6 +15,7 @@ FP8X4 = mybir.dt.float8_e4m3fn_x4
 FP4X4 = mybir.dt.float4_e2m1fn_x4
 ACT = mybir.ActivationFunctionType
 MULT = mybir.AluOpType.mult
+ADD = mybir.AluOpType.add
 
 P = 128
 PACK = 4
@@ -27,17 +28,17 @@ HALF = J // 2
 QUARTER = J // 4
 SLOT = QUARTER + J
 CHUNK = 128
-GROUPS = [(0, 256), (256, 256), (512, 256), (768, 128), (896, 128)]
-VECTOR_EMPTIES = (2, 3, 4)
+GROUPS = [(0, 256), (256, 256), (512, 128), (640, 128), (768, 128), (896, 128)]
+VECTOR_EMPTIES = (3, 4, 5)
 WU_SPLIT = P // 2
-WD_SPLIT = 3 * P // 4
+WD_SPLIT = 256
 
 
 def tile_list_tanh_bias_kernel(tc, xT, wgt, wg_words, wg_scales, wu, wd, b, offs, out):
     nc = tc.nc
     with ExitStack() as ctx:
         sb = ctx.enter_context(tc.tile_pool(name="sb", bufs=1))
-        psum = [ctx.enter_context(tc.psum_pool(name="psum%d" % h, bufs=PACK)) for h in range(2)]
+        psum = [ctx.enter_context(tc.psum_pool(name="psum%d" % h, bufs=n)) for h, n in enumerate((3, 4, 1))]
 
         def tile(name, shape, dtype, tag=None):
             return sb.tile(shape, dtype, name=name, tag=tag or name, align_bytes=64)
@@ -52,17 +53,18 @@ def tile_list_tanh_bias_kernel(tc, xT, wgt, wg_words, wg_scales, wu, wd, b, offs
         wgt_sb = shared[:, 1, QUARTER:SLOT]
         planes = [[tile("plane%d%d" % (a, i), [P, T], F32) for i in range(PACK)] for a in range(PASSES)]
         wu_raw = [tile("wu_raw%d" % a, [P, PACK, R], F32) for a in range(PASSES)]
-        wd_raw = tile("wd_raw", [P, PACK, N], F32)
+        wd_tile = tile("wd_tile", [P, 2 * CHUNK + PACK * N], F32)
+        wd_raw = wd_tile[:, 2 * CHUNK :].rearrange("p (i n) -> p i n", i=PACK)
         bias = tile("bias", [P, PACK], F32)
 
         nc.vector.memset(wg_scales_raw[:].rearrange("p a r -> p (a r)").bitcast(I32), 0)
         nc.sync.dma_start(offsets[:], offs)
         nc.sync.dma_start(out=wg_words_raw[:].bitcast(I32), in_=wg_words.rearrange("a p n -> p a n").bitcast(I32))
         nc.sync.dma_start(out=wgt_sb[:, 0:HALF], in_=wgt[:, 0:HALF])
-        for q in range(P // QUADRANT):
+        for r in range(4):
             nc.sync.dma_start(
-                out=wg_scales_raw[QUADRANT * q : QUADRANT * q + 4, :, :].bitcast(I32),
-                in_=wg_scales[:, 4 * q : 4 * q + 4, :].rearrange("a r n -> r a n").bitcast(I32),
+                out=wg_scales_raw[r:P:QUADRANT, :, :].bitcast(I32),
+                in_=wg_scales[:, r:16:4, :].rearrange("a q n -> q a n").bitcast(I32),
             )
         for a in range(PASSES):
             rows = xT[a * PASS_K : (a + 1) * PASS_K, :].rearrange("(p i) t -> p i t", i=PACK)
@@ -73,8 +75,9 @@ def tile_list_tanh_bias_kernel(tc, xT, wgt, wg_words, wg_scales, wu, wd, b, offs
         for a in range(PASSES):
             rows = wu[a * PASS_K : (a + 1) * PASS_K, :].rearrange("(p i) r -> p i r", i=PACK)
             nc.sync.dma_start(out=wu_raw[a][:], in_=rows)
-        nc.sync.dma_start(out=wd_raw[:], in_=wd.rearrange("(p i) n -> p i n", i=PACK))
-        nc.sync.dma_start(out=bias[:], in_=b.rearrange("(p t) -> p t", t=PACK))
+        nc.sync.dma_start(out=wd_raw, in_=wd.rearrange("(p i) n -> p i n", i=PACK))
+        with nc.allow_non_contiguous_dma(reason="one bias value for each partition and result"):
+            nc.sync.dma_start(out=bias[:], in_=b.rearrange("(t p) -> p t", t=PACK))
 
         nc.vector.tensor_copy(
             out=wg_codes[:].bitcast(U16),
@@ -91,10 +94,11 @@ def tile_list_tanh_bias_kernel(tc, xT, wgt, wg_words, wg_scales, wu, wd, b, offs
             [shared[:, 2 : PACK + 2, 0:HALF], shared[:, 0:PACK, 0:HALF]],
         ]
         wu_bf16 = [tile("wu_bf16_%d" % a, [P, PACK, P, PACK], BF16)[:] for a in range(PASSES)]
-        after_wu = tile("after_wu", [P, (PACK + 2) * HALF], F32, tag="wu_raw1")
+        wd_start = (PACK + 2) * HALF - 2 * WD_SPLIT
+        after_wu = tile("after_wu", [P, wd_start + 2 * N], F32, tag="wu_raw1")
         xg_bf16 = [
             [tile("xg_bf16_0%d" % h, [P, HALF, PACK], BF16)[:] for h in range(2)],
-            [tile("xg_bf16_10", [P, HALF, PACK], BF16)[:], after_wu[:, PACK * HALF :].bitcast(BF16).rearrange("p (j i) -> p j i", i=PACK)],
+            [tile("xg_bf16_10", [P, HALF, PACK], BF16)[:], after_wu[:, PACK * HALF : (PACK + 2) * HALF].bitcast(BF16).rearrange("p (j i) -> p j i", i=PACK)],
         ]
         xg_codes = [tile("xg_codes%d" % a, [P, J], U32) for a in range(PASSES)]
         xg_scale = [tile("xg_scale%d" % a, [P, J], U8) for a in range(PASSES)]
@@ -135,7 +139,7 @@ def tile_list_tanh_bias_kernel(tc, xT, wgt, wg_words, wg_scales, wu, wd, b, offs
 
         wu_codes = [tile("wu_codes%d" % a, [P, R], U32) for a in range(PASSES)]
         wu_scale = [tile("wu_scale%d" % a, [P, R], U8) for a in range(PASSES)]
-        wd_bf16 = tile("wd_bf16", [P, PACK, P, PACK], BF16)[:]
+        wd_bf16 = after_wu[:, wd_start:].bitcast(BF16)
 
         def quantize_wu(a):
             quantize(wu_codes[a][:], wu_scale[a][:], wu_bf16[a].rearrange("p t m i -> p (t m i)"))
@@ -179,17 +183,18 @@ def tile_list_tanh_bias_kernel(tc, xT, wgt, wg_words, wg_scales, wu, wd, b, offs
             after_wu[:, 0 : PACK * HALF].rearrange("p (t j) -> p t j", t=PACK),
             tile("tanh_ga1", [P, PACK, HALF], F32)[:],
         ]
-        h_bf16 = [tile("h_bf16_%d" % g, [P, width, PACK], BF16) for g, (j0, width) in enumerate(GROUPS)]
+        h_bf16 = [g != 1 and tile("h_bf16_%d" % g, [P, width, PACK], BF16)[:] for g, (j0, width) in enumerate(GROUPS)]
         h_codes = [tile("h_codes%d" % g, [P, width], U32) for g, (j0, width) in enumerate(GROUPS)]
+        h_bf16[1] = wd_tile[:, 0 : 4 * CHUNK].bitcast(BF16).rearrange("p (j t) -> p j t", t=PACK)
         h_scale = [tile("h_scale%d" % g, [P, width], U8) for g, (j0, width) in enumerate(GROUPS)]
         result = [
             [tile("result%d%d" % (g, pair), [P, 2, width], F32) for pair in range(2)]
             for g, (j0, width) in enumerate(GROUPS)
         ]
-        out_rows = out.rearrange("(p t) j -> p t j", t=PACK)
+        out_rows = out.rearrange("(t p) j -> p t j", t=PACK)
 
         ga = [
-            [psum[h].tile([P, HALF], F32, name="ga%d%d" % (h, t), tag="bank") for t in range(PACK)]
+            [psum[2 if (h, t) == (0, 3) else h].tile([P, HALF], F32, name="ga%d%d" % (h, t), tag="bank") for t in range(PACK)]
             for h in range(2)
         ]
 
@@ -238,12 +243,12 @@ def tile_list_tanh_bias_kernel(tc, xT, wgt, wg_words, wg_scales, wu, wd, b, offs
             )
 
         def quantize_h(g):
-            quantize(h_codes[g][:], h_scale[g][:], h_bf16[g][:].rearrange("p j t -> p (j t)"))
+            quantize(h_codes[g][:], h_scale[g][:], h_bf16[g].rearrange("p j t -> p (j t)"))
 
         def down_product(g):
             j0, width = GROUPS[g]
             for pair in range(2):
-                y = psum[1 if width == QUARTER else 0].tile([P, 2, width], F32, name="y", tag="bank")
+                y = psum[((2, 1), (1, 1), (2, 1), (1, 1), (0, 0), (0, 1))[g][pair]].tile([P, 2, width], F32, name="y", tag="bank")
                 for v in range(2):
                     t = 2 * pair + v
                     nc.tensor.matmul_mx(
@@ -268,31 +273,45 @@ def tile_list_tanh_bias_kernel(tc, xT, wgt, wg_words, wg_scales, wu, wd, b, offs
         gate_pass(1, 0)
         gate_pass(0, 1)
         gate_tanh(0)
-        interleave_weight(nc.scalar.copy, wd_raw[:], wd_bf16, 0, WD_SPLIT)
-        interleave_weight(nc.vector.tensor_copy, wd_raw[:], wd_bf16, WD_SPLIT, P)
+        nc.scalar.copy(
+            out=wd_bf16.rearrange("p (c e i) -> p c i e", e=RUN, i=PACK)[:, WD_SPLIT // RUN :],
+            in_=wd_raw.rearrange("p i (c e) -> p c i e", e=RUN)[:, WD_SPLIT // RUN :],
+        )
+        nc.gpsimd.tensor_scalar(
+            wd_bf16[:, 0 : PACK * WD_SPLIT].rearrange("p (n i) -> p n i", i=PACK),
+            wd_raw[:, :, 0:WD_SPLIT].rearrange("p i n -> p n i"),
+            1.0,
+            0.0,
+            MULT,
+            ADD,
+        )
 
         ub = [up_product(chunk) for chunk in range(3)]
         gate_pass(1, 1)
         gate_tanh(1)
-        ub.append(up_product(3))
         form_h(0, ub[0])
-        ub.append(up_product(4))
+        ub.append(up_product(3))
         form_h(1, ub[1])
-        ub.append(up_product(5))
+        ub.append(up_product(4))
         form_h(2, ub[2])
         quantize_h(0)
-        ub.append(up_product(6))
-        form_h(3, ub[3])
-        quantize(wd_codes[:], wd_scale[:], wd_bf16.rearrange("p t m i -> p (t m i)"))
-        quantize_h(1)
+        quantize(wd_codes[:], wd_scale[:], wd_bf16)
         down_product(0)
+        ub.append(up_product(5))
+        form_h(3, ub[3])
+        ub.append(up_product(6))
+        form_h(4, ub[4])
+        quantize_h(1)
         down_product(1)
         ub.append(up_product(7))
-        for chunk in range(4, 7):
-            form_h(chunk, ub[chunk])
+        form_h(5, ub[5])
         quantize_h(2)
-        form_h(7, ub[7])
+        down_product(2)
+        form_h(6, ub[6])
         quantize_h(3)
+        form_h(7, ub[7])
         quantize_h(4)
-        for g in range(2, len(GROUPS)):
-            down_product(g)
+        down_product(3)
+        quantize_h(5)
+        down_product(4)
+        down_product(5)

@@ -198,18 +198,17 @@ def tile_list_tanh_bias_kernel(tc, xT, wgt, wg_words, wg_scales, wu, wd, b, offs
             for h in range(2)
         ]
 
-        def gate_pass(h, a):
+        def gate_pass(h, t, a, start):
             cols = slice(h * HALF, (h + 1) * HALF)
-            for t in range(PACK):
-                nc.tensor.matmul_mx(
-                    out=ga[h][t][:],
-                    lhsT=wg_codes[:, a, t, :].bitcast(FP4X4),
-                    lhsT_scale=wg_scale[:, a, t, :],
-                    rhs=xg_codes[a][:, cols].bitcast(FP8X4),
-                    rhs_scale=xg_scale[a][:, cols],
-                    start=(a == 0),
-                    stop=(a == PASSES - 1),
-                )
+            nc.tensor.matmul_mx(
+                out=ga[h][t][:],
+                lhsT=wg_codes[:, a, t, :].bitcast(FP4X4),
+                lhsT_scale=wg_scale[:, a, t, :],
+                rhs=xg_codes[a][:, cols].bitcast(FP8X4),
+                rhs_scale=xg_scale[a][:, cols],
+                start=start,
+                stop=not start,
+            )
 
         def gate_tanh(h):
             for t in range(PACK):
@@ -269,9 +268,11 @@ def tile_list_tanh_bias_kernel(tc, xT, wgt, wg_words, wg_scales, wu, wd, b, offs
                         nc.scalar.activation(out=dst, in_=y[:, v, :], func=ACT.Identity, bias=bias[:, t : t + 1])
                 nc.sync.dma_start(out=out_rows[:, 2 * pair : 2 * pair + 2, j0 : j0 + width], in_=result[g][pair][:])
 
-        gate_pass(0, 0)
-        gate_pass(1, 0)
-        gate_pass(0, 1)
+        for t in range(PACK):
+            gate_pass(1, t, 0, True)
+        for t in range(PACK):
+            gate_pass(0, t, 1, True)
+            gate_pass(0, t, 0, False)
         gate_tanh(0)
         nc.scalar.copy(
             out=wd_bf16.rearrange("p (c e i) -> p c i e", e=RUN, i=PACK)[:, WD_SPLIT // RUN :],
@@ -287,7 +288,8 @@ def tile_list_tanh_bias_kernel(tc, xT, wgt, wg_words, wg_scales, wu, wd, b, offs
         )
 
         ub = [up_product(chunk) for chunk in range(3)]
-        gate_pass(1, 1)
+        for t in range(PACK):
+            gate_pass(1, t, 1, False)
         gate_tanh(1)
         form_h(0, ub[0])
         ub.append(up_product(3))

@@ -31,7 +31,7 @@ CHUNK = 128
 GROUPS = [(0, 256), (256, 256), (512, 128), (640, 128), (768, 128), (896, 128)]
 VECTOR_EMPTIES = (3, 4, 5)
 WU_SPLIT = P // 2
-WD_SPLIT = 256
+WD_SPLIT = 192
 
 
 def tile_list_tanh_bias_kernel(tc, xT, wgt, wg_words, wg_scales, wu, wd, b, offs, out):
@@ -259,12 +259,13 @@ def tile_list_tanh_bias_kernel(tc, xT, wgt, wg_words, wg_scales, wu, wd, b, offs
                         start=True,
                         stop=True,
                     )
-                for v in range(2):
-                    t = 2 * pair + v
-                    dst = result[g][pair][:, v, :]
-                    if g in VECTOR_EMPTIES and pair == 1:
-                        nc.vector.tensor_scalar_add(dst, y[:, v, :], bias[:, t : t + 1])
-                    else:
+                if g in VECTOR_EMPTIES and pair == 1:
+                    both = bias[:, 2:4].unsqueeze(2).to_broadcast([P, 2, width])
+                    nc.vector.tensor_tensor(result[g][pair][:], y[:], both, ADD)
+                else:
+                    for v in range(2):
+                        t = 2 * pair + v
+                        dst = result[g][pair][:, v, :]
                         nc.scalar.activation(out=dst, in_=y[:, v, :], func=ACT.Identity, bias=bias[:, t : t + 1])
                 nc.sync.dma_start(out=out_rows[:, 2 * pair : 2 * pair + 2, j0 : j0 + width], in_=result[g][pair][:])
 
@@ -313,7 +314,7 @@ def tile_list_tanh_bias_kernel(tc, xT, wgt, wg_words, wg_scales, wu, wd, b, offs
         quantize_h(3)
         form_h(7, ub[7])
         quantize_h(4)
-        down_product(3)
         quantize_h(5)
+        down_product(3)
         down_product(4)
         down_product(5)

@@ -31,6 +31,7 @@ CHUNK = 128
 GROUPS = [(0, 256), (256, 256), (512, 128), (640, 128), (768, 128), (896, 128)]
 VECTOR_EMPTIES = (3, 4, 5)
 WU_SPLIT = P // 2
+WGT_AHEAD = 3 * QUARTER
 WD_SPLIT = 192
 
 
@@ -59,8 +60,7 @@ def tile_list_tanh_bias_kernel(tc, xT, wgt, wg_words, wg_scales, wu, wd, b, offs
 
         nc.vector.memset(wg_scales_raw[:].rearrange("p a r -> p (a r)").bitcast(I32), 0)
         nc.sync.dma_start(offsets[:], offs)
-        nc.sync.dma_start(out=wg_words_raw[:].bitcast(I32), in_=wg_words.rearrange("a p n -> p a n").bitcast(I32))
-        nc.sync.dma_start(out=wgt_sb[:, 0:HALF], in_=wgt[:, 0:HALF])
+        nc.sync.dma_start(out=wgt_sb[:, 0:WGT_AHEAD], in_=wgt[:, 0:WGT_AHEAD])
         for r in range(4):
             nc.sync.dma_start(
                 out=wg_scales_raw[r:P:QUADRANT, :, :].bitcast(I32),
@@ -71,7 +71,9 @@ def tile_list_tanh_bias_kernel(tc, xT, wgt, wg_words, wg_scales, wu, wd, b, offs
             for i in range(PACK):
                 nc.sync.dma_start(out=planes[a][i][:], in_=rows[:, i, :])
                 if (a, i) == (0, 0):
-                    nc.sync.dma_start(out=wgt_sb[:, HALF:J], in_=wgt[:, HALF:J])
+                    nc.sync.dma_start(out=wgt_sb[:, WGT_AHEAD:J], in_=wgt[:, WGT_AHEAD:J])
+                if (a, i) == (1, 0):
+                    nc.sync.dma_start(out=wg_words_raw[:].bitcast(I32), in_=wg_words.rearrange("a p n -> p a n").bitcast(I32))
         for a in range(PASSES):
             rows = wu[a * PASS_K : (a + 1) * PASS_K, :].rearrange("(p i) r -> p i r", i=PACK)
             nc.sync.dma_start(out=wu_raw[a][:], in_=rows)
@@ -79,10 +81,7 @@ def tile_list_tanh_bias_kernel(tc, xT, wgt, wg_words, wg_scales, wu, wd, b, offs
         with nc.allow_non_contiguous_dma(reason="one bias value for each partition and result"):
             nc.sync.dma_start(out=bias[:], in_=b.rearrange("(t p) -> p t", t=PACK))
 
-        nc.vector.tensor_copy(
-            out=wg_codes[:].bitcast(U16),
-            in_=wg_words_raw[:].bitcast(U16).rearrange("p a (m t) -> p a t m", t=PACK),
-        )
+
         nc.vector.tensor_copy(
             out=wg_scale[:],
             in_=wg_scales_raw[:].rearrange("p a (m t) -> p a t m", t=PACK),
@@ -106,7 +105,7 @@ def tile_list_tanh_bias_kernel(tc, xT, wgt, wg_words, wg_scales, wu, wd, b, offs
         def gather(a, i, j0, width):
             h, c0 = divmod(j0, HALF)
             nc.vector.tensor_tensor(
-                xg_first[:, i, :] if width == J else xg[a][h][:, i, c0 : c0 + width],
+                xg_first[:, i, j0 : j0 + width] if a == 0 else xg[a][h][:, i, c0 : c0 + width],
                 planes[a][i][:].indirect(offsets[:, j0 // LIST_ROWS : (j0 + width) // LIST_ROWS]),
                 wgt_sb[:, j0 : j0 + width],
                 MULT,
@@ -145,13 +144,20 @@ def tile_list_tanh_bias_kernel(tc, xT, wgt, wg_words, wg_scales, wu, wd, b, offs
             quantize(wu_codes[a][:], wu_scale[a][:], wu_bf16[a].rearrange("p t m i -> p (t m i)"))
 
         for i in range(PACK):
-            if i in (0, PACK - 1):
+            if i == 0:
+                gather(0, i, 0, WGT_AHEAD)
+                gather(0, i, WGT_AHEAD, J - WGT_AHEAD)
+            elif i == PACK - 1:
                 gather(0, i, 0, HALF)
                 gather(0, i, HALF, HALF)
             else:
                 gather(0, i, 0, J)
         for h in range(2):
             interleave_xg(activation_copy, 0, h * HALF, HALF)
+        nc.scalar.copy(
+            out=wg_codes[:].bitcast(U16),
+            in_=wg_words_raw[:].bitcast(U16).rearrange("p a (m t) -> p a t m", t=PACK),
+        )
 
         gather(1, 0, 0, HALF)
         gather(1, 0, HALF, HALF)

@@ -26,12 +26,15 @@ QUADRANT = 32
 RUN = 4
 HALF = J // 2
 QUARTER = J // 4
-SLOT = QUARTER + J
 CHUNK = 128
 GROUPS = [(0, 256), (256, 256), (512, 128), (640, 128), (768, 128), (896, 128)]
+DOWN_POOLS = ((2, 1), (1, 1), (2, 1), (1, 1), (0, 0), (0, 1))
 VECTOR_EMPTIES = (3, 4, 5)
-WU_SPLIT = P // 2
 WGT_AHEAD = 3 * QUARTER
+FIRST = 192
+WGT_START = HALF - FIRST
+SLOT = WGT_START + J
+WU_SPLIT = 48
 WD_SPLIT = 192
 
 
@@ -39,7 +42,7 @@ def tile_list_tanh_bias_kernel(tc, xT, wgt, wg_words, wg_scales, wu, wd, b, offs
     nc = tc.nc
     with ExitStack() as ctx:
         sb = ctx.enter_context(tc.tile_pool(name="sb", bufs=1))
-        psum = [ctx.enter_context(tc.psum_pool(name="psum%d" % h, bufs=n)) for h, n in enumerate((3, 4, 1))]
+        psum = [ctx.enter_context(tc.psum_pool(name="psum%d" % k, bufs=n)) for k, n in enumerate((3, 4, 1))]
 
         def tile(name, shape, dtype, tag=None):
             return sb.tile(shape, dtype, name=name, tag=tag or name, align_bytes=64)
@@ -51,7 +54,7 @@ def tile_list_tanh_bias_kernel(tc, xT, wgt, wg_words, wg_scales, wu, wd, b, offs
         wg_scale = tile("wg_scale", [P, PASSES, PACK, P], U8)
 
         shared = tile("shared", [P, PACK + 2, SLOT], F32)
-        wgt_sb = shared[:, 1, QUARTER:SLOT]
+        wgt_sb = shared[:, 1, WGT_START:SLOT]
         planes = [[tile("plane%d%d" % (a, i), [P, T], F32) for i in range(PACK)] for a in range(PASSES)]
         wu_raw = [tile("wu_raw%d" % a, [P, PACK, R], F32) for a in range(PASSES)]
         wd_tile = tile("wd_tile", [P, 2 * CHUNK + PACK * N], F32)
@@ -73,14 +76,16 @@ def tile_list_tanh_bias_kernel(tc, xT, wgt, wg_words, wg_scales, wu, wd, b, offs
                 if (a, i) == (0, 0):
                     nc.sync.dma_start(out=wgt_sb[:, WGT_AHEAD:J], in_=wgt[:, WGT_AHEAD:J])
                 if (a, i) == (1, 0):
-                    nc.sync.dma_start(out=wg_words_raw[:].bitcast(I32), in_=wg_words.rearrange("a p n -> p a n").bitcast(I32))
+                    nc.sync.dma_start(
+                        out=wg_words_raw[:].bitcast(I32),
+                        in_=wg_words.rearrange("a p n -> p a n").bitcast(I32),
+                    )
         for a in range(PASSES):
             rows = wu[a * PASS_K : (a + 1) * PASS_K, :].rearrange("(p i) r -> p i r", i=PACK)
             nc.sync.dma_start(out=wu_raw[a][:], in_=rows)
         nc.sync.dma_start(out=wd_raw, in_=wd.rearrange("(p i) n -> p i n", i=PACK))
         with nc.allow_non_contiguous_dma(reason="one bias value for each partition and result"):
             nc.sync.dma_start(out=bias[:], in_=b.rearrange("(t p) -> p t", t=PACK))
-
 
         nc.vector.tensor_copy(
             out=wg_scale[:],
@@ -89,23 +94,24 @@ def tile_list_tanh_bias_kernel(tc, xT, wgt, wg_words, wg_scales, wu, wd, b, offs
 
         xg_first = tile("xg_first", [P, PACK, J], F32)
         xg = [
-            [xg_first[:, :, h * HALF : (h + 1) * HALF] for h in range(2)],
+            [xg_first[:, :, half * HALF : (half + 1) * HALF] for half in range(2)],
             [shared[:, 2 : PACK + 2, 0:HALF], shared[:, 0:PACK, 0:HALF]],
         ]
         wu_bf16 = [tile("wu_bf16_%d" % a, [P, PACK, P, PACK], BF16)[:] for a in range(PASSES)]
         wd_start = (PACK + 2) * HALF - 2 * WD_SPLIT
         after_wu = tile("after_wu", [P, wd_start + 2 * N], F32, tag="wu_raw1")
+        xg_last = after_wu[:, PACK * HALF : (PACK + 2) * HALF].bitcast(BF16)
         xg_bf16 = [
-            [tile("xg_bf16_0%d" % h, [P, HALF, PACK], BF16)[:] for h in range(2)],
-            [tile("xg_bf16_10", [P, HALF, PACK], BF16)[:], after_wu[:, PACK * HALF : (PACK + 2) * HALF].bitcast(BF16).rearrange("p (j i) -> p j i", i=PACK)],
+            [tile("xg_bf16_0%d" % half, [P, HALF, PACK], BF16)[:] for half in range(2)],
+            [tile("xg_bf16_10", [P, HALF, PACK], BF16)[:], xg_last.rearrange("p (j i) -> p j i", i=PACK)],
         ]
         xg_codes = [tile("xg_codes%d" % a, [P, J], U32) for a in range(PASSES)]
         xg_scale = [tile("xg_scale%d" % a, [P, J], U8) for a in range(PASSES)]
 
         def gather(a, i, j0, width):
-            h, c0 = divmod(j0, HALF)
+            half, c0 = divmod(j0, HALF)
             nc.vector.tensor_tensor(
-                xg_first[:, i, j0 : j0 + width] if a == 0 else xg[a][h][:, i, c0 : c0 + width],
+                xg_first[:, i, j0 : j0 + width] if a == 0 else xg[a][half][:, i, c0 : c0 + width],
                 planes[a][i][:].indirect(offsets[:, j0 // LIST_ROWS : (j0 + width) // LIST_ROWS]),
                 wgt_sb[:, j0 : j0 + width],
                 MULT,
@@ -115,19 +121,19 @@ def tile_list_tanh_bias_kernel(tc, xT, wgt, wg_words, wg_scales, wu, wd, b, offs
             nc.scalar.activation(out=out, in_=in_, func=ACT.Copy)
 
         def interleave_xg(copy, a, j0, width):
-            h, c0 = divmod(j0, HALF)
+            half, c0 = divmod(j0, HALF)
             copy(
-                out=xg_bf16[a][h][:, c0 : c0 + width, :].rearrange("p (c e) i -> p c i e", e=RUN),
-                in_=xg[a][h][:, :, c0 : c0 + width].rearrange("p i (c e) -> p c i e", e=RUN),
+                out=xg_bf16[a][half][:, c0 : c0 + width, :].rearrange("p (c e) i -> p c i e", e=RUN),
+                in_=xg[a][half][:, :, c0 : c0 + width].rearrange("p i (c e) -> p c i e", e=RUN),
             )
 
         def quantize(codes, scale, src):
             nc.vector.quantize_mx(out=codes.bitcast(FP8X4), scales=scale, in_=src)
 
         def quantize_xg(a, j0, width):
-            h, c0 = divmod(j0, HALF)
+            half, c0 = divmod(j0, HALF)
             cols = slice(j0, j0 + width)
-            src = xg_bf16[a][h][:, c0 : c0 + width, :].rearrange("p j i -> p (j i)")
+            src = xg_bf16[a][half][:, c0 : c0 + width, :].rearrange("p j i -> p (j i)")
             quantize(xg_codes[a][:, cols], xg_scale[a][:, cols], src)
 
         def interleave_weight(copy, raw, dst, m0, m1):
@@ -152,8 +158,8 @@ def tile_list_tanh_bias_kernel(tc, xT, wgt, wg_words, wg_scales, wu, wd, b, offs
                 gather(0, i, HALF, HALF)
             else:
                 gather(0, i, 0, J)
-        for h in range(2):
-            interleave_xg(activation_copy, 0, h * HALF, HALF)
+        for half in range(2):
+            interleave_xg(activation_copy, 0, half * HALF, HALF)
         nc.scalar.copy(
             out=wg_codes[:].bitcast(U16),
             in_=wg_words_raw[:].bitcast(U16).rearrange("p a (m t) -> p a t m", t=PACK),
@@ -165,9 +171,9 @@ def tile_list_tanh_bias_kernel(tc, xT, wgt, wg_words, wg_scales, wu, wd, b, offs
         quantize_xg(0, 0, HALF)
         gather(1, 2, 0, HALF)
         quantize_xg(0, HALF, HALF)
-        for quarter in range(2):
-            gather(1, 3, quarter * QUARTER, QUARTER)
-            interleave_xg(nc.scalar.copy, 1, quarter * QUARTER, QUARTER)
+        for j0, width in ((0, FIRST), (FIRST, HALF - FIRST)):
+            gather(1, 3, j0, width)
+            interleave_xg(nc.scalar.copy, 1, j0, width)
 
         interleave_weight(nc.scalar.copy, wu_raw[0][:], wu_bf16[0], 0, WU_SPLIT)
         interleave_weight(nc.scalar.copy, wu_raw[1][:], wu_bf16[1], 0, P)
@@ -189,9 +195,12 @@ def tile_list_tanh_bias_kernel(tc, xT, wgt, wg_words, wg_scales, wu, wd, b, offs
             after_wu[:, 0 : PACK * HALF].rearrange("p (t j) -> p t j", t=PACK),
             tile("tanh_ga1", [P, PACK, HALF], F32)[:],
         ]
-        h_bf16 = [g != 1 and tile("h_bf16_%d" % g, [P, width, PACK], BF16)[:] for g, (j0, width) in enumerate(GROUPS)]
+        h_on_wd = wd_tile[:, 0 : 4 * CHUNK].bitcast(BF16).rearrange("p (j t) -> p j t", t=PACK)
+        h_bf16 = [
+            h_on_wd if g == 1 else tile("h_bf16_%d" % g, [P, width, PACK], BF16)[:]
+            for g, (j0, width) in enumerate(GROUPS)
+        ]
         h_codes = [tile("h_codes%d" % g, [P, width], U32) for g, (j0, width) in enumerate(GROUPS)]
-        h_bf16[1] = wd_tile[:, 0 : 4 * CHUNK].bitcast(BF16).rearrange("p (j t) -> p j t", t=PACK)
         h_scale = [tile("h_scale%d" % g, [P, width], U8) for g, (j0, width) in enumerate(GROUPS)]
         result = [
             [tile("result%d%d" % (g, pair), [P, 2, width], F32) for pair in range(2)]
@@ -199,15 +208,16 @@ def tile_list_tanh_bias_kernel(tc, xT, wgt, wg_words, wg_scales, wu, wd, b, offs
         ]
         out_rows = out.rearrange("(t p) j -> p t j", t=PACK)
 
+        gate_pools = ((0, 0, 0, 2), (1, 1, 1, 1))
         ga = [
-            [psum[2 if (h, t) == (0, 3) else h].tile([P, HALF], F32, name="ga%d%d" % (h, t), tag="bank") for t in range(PACK)]
-            for h in range(2)
+            [psum[k].tile([P, HALF], F32, name="ga%d%d" % (half, t), tag="bank") for t, k in enumerate(pools)]
+            for half, pools in enumerate(gate_pools)
         ]
 
-        def gate_pass(h, t, a, start):
-            cols = slice(h * HALF, (h + 1) * HALF)
+        def gate_pass(half, t, a, start):
+            cols = slice(half * HALF, (half + 1) * HALF)
             nc.tensor.matmul_mx(
-                out=ga[h][t][:],
+                out=ga[half][t][:],
                 lhsT=wg_codes[:, a, t, :].bitcast(FP4X4),
                 lhsT_scale=wg_scale[:, a, t, :],
                 rhs=xg_codes[a][:, cols].bitcast(FP8X4),
@@ -216,9 +226,9 @@ def tile_list_tanh_bias_kernel(tc, xT, wgt, wg_words, wg_scales, wu, wd, b, offs
                 stop=not start,
             )
 
-        def gate_tanh(h):
+        def gate_tanh(half):
             for t in range(PACK):
-                nc.scalar.activation(out=tanh_ga[h][:, t, :], in_=ga[h][t][:], func=ACT.Tanh)
+                nc.scalar.activation(out=tanh_ga[half][:, t, :], in_=ga[half][t][:], func=ACT.Tanh)
 
         def up_product(chunk):
             cols = slice(chunk * CHUNK, (chunk + 1) * CHUNK)
@@ -239,11 +249,11 @@ def tile_list_tanh_bias_kernel(tc, xT, wgt, wg_words, wg_scales, wu, wd, b, offs
         def form_h(chunk, ub):
             g = max(k for k, (j0, width) in enumerate(GROUPS) if j0 <= chunk * CHUNK)
             in_group = chunk * CHUNK - GROUPS[g][0]
-            h, in_half = divmod(chunk * CHUNK, HALF)
+            half, in_half = divmod(chunk * CHUNK, HALF)
             nc.vector.tensor_tensor(
                 h_bf16[g][:, in_group : in_group + CHUNK, :].rearrange("p (c e) t -> p c t e", e=RUN),
                 ub[:].rearrange("p t (c e) -> p c t e", e=RUN),
-                tanh_ga[h][:, :, in_half : in_half + CHUNK].rearrange("p t (c e) -> p c t e", e=RUN),
+                tanh_ga[half][:, :, in_half : in_half + CHUNK].rearrange("p t (c e) -> p c t e", e=RUN),
                 MULT,
             )
 
@@ -253,7 +263,7 @@ def tile_list_tanh_bias_kernel(tc, xT, wgt, wg_words, wg_scales, wu, wd, b, offs
         def down_product(g):
             j0, width = GROUPS[g]
             for pair in range(2):
-                y = psum[((2, 1), (1, 1), (2, 1), (1, 1), (0, 0), (0, 1))[g][pair]].tile([P, 2, width], F32, name="y", tag="bank")
+                y = psum[DOWN_POOLS[g][pair]].tile([P, 2, width], F32, name="y", tag="bank")
                 for v in range(2):
                     t = 2 * pair + v
                     nc.tensor.matmul_mx(

@@ -35,7 +35,7 @@ FIRST = 192
 WGT_START = HALF - FIRST
 SLOT = WGT_START + J
 WU_SPLIT = 48
-WD_SPLIT = 192
+WD_SPLIT = 320
 
 
 def tile_list_tanh_bias_kernel(tc, xT, wgt, wg_words, wg_scales, wu, wd, b, offs, out):
@@ -296,8 +296,8 @@ def tile_list_tanh_bias_kernel(tc, xT, wgt, wg_words, wg_scales, wu, wd, b, offs
             in_=wd_raw.rearrange("p i (c e) -> p c i e", e=RUN)[:, WD_SPLIT // RUN :],
         )
         nc.gpsimd.tensor_scalar(
-            wd_bf16[:, 0 : PACK * WD_SPLIT].rearrange("p (n i) -> p n i", i=PACK),
-            wd_raw[:, :, 0:WD_SPLIT].rearrange("p i n -> p n i"),
+            wd_bf16[:, 0 : PACK * WD_SPLIT].rearrange("p (c e i) -> p c i e", e=RUN, i=PACK),
+            wd_raw[:, :, 0:WD_SPLIT].rearrange("p i (c e) -> p c i e", e=RUN),
             1.0,
             0.0,
             MULT,

from contextlib import ExitStack

import concourse.mybir as mybir

K, R, N, T, J = 1024, 512, 512, 2048, 1024
FLOPS = 2 * J * (2 * K * R + R * N)

F32 = mybir.dt.float32
BF16 = mybir.dt.bfloat16
I32 = mybir.dt.int32
U32 = mybir.dt.uint32
U16 = mybir.dt.uint16
U8 = mybir.dt.uint8
FP8X4 = mybir.dt.float8_e4m3fn_x4
FP4X4 = mybir.dt.float4_e2m1fn_x4
ACT = mybir.ActivationFunctionType
MULT = mybir.AluOpType.mult
ADD = mybir.AluOpType.add

P = 128
PACK = 4
PASS_K = P * PACK
PASSES = K // PASS_K
LIST_ROWS = 16
QUADRANT = 32
RUN = 4
HALF = J // 2
QUARTER = J // 4
CHUNK = 128
GROUPS = [(0, 256), (256, 256), (512, 128), (640, 128), (768, 128), (896, 128)]
DOWN_POOLS = ((2, 1), (1, 1), (2, 1), (1, 1), (0, 0), (0, 1))
VECTOR_EMPTIES = (3, 4, 5)
WGT_AHEAD = 3 * QUARTER
FIRST = 192
WGT_START = HALF - FIRST
SLOT = WGT_START + J
WU_SPLIT = 48
WD_SPLIT = 320


def tile_list_tanh_bias_kernel(tc, xT, wgt, wg_words, wg_scales, wu, wd, b, offs, out):
    nc = tc.nc
    with ExitStack() as ctx:
        sb = ctx.enter_context(tc.tile_pool(name="sb", bufs=1))
        psum = [ctx.enter_context(tc.psum_pool(name="psum%d" % k, bufs=n)) for k, n in enumerate((3, 4, 1))]

        def tile(name, shape, dtype, tag=None):
            return sb.tile(shape, dtype, name=name, tag=tag or name, align_bytes=64)

        offsets = sb.tile([P, J // LIST_ROWS], U16, name="offsets")
        wg_words_raw = tile("wg_words_raw", [P, PASSES, 2 * R], U8)
        wg_scales_raw = tile("wg_scales_raw", [P, PASSES, R], U8)
        wg_codes = tile("wg_codes", [P, PASSES, PACK, 2 * P], U8)
        wg_scale = tile("wg_scale", [P, PASSES, PACK, P], U8)

        shared = tile("shared", [P, PACK + 2, SLOT], F32)
        wgt_sb = shared[:, 1, WGT_START:SLOT]
        planes = [[tile("plane%d%d" % (a, i), [P, T], F32) for i in range(PACK)] for a in range(PASSES)]
        wu_raw = [tile("wu_raw%d" % a, [P, PACK, R], F32) for a in range(PASSES)]
        wd_tile = tile("wd_tile", [P, 2 * CHUNK + PACK * N], F32)
        wd_raw = wd_tile[:, 2 * CHUNK :].rearrange("p (i n) -> p i n", i=PACK)
        bias = tile("bias", [P, PACK], F32)

        nc.vector.memset(wg_scales_raw[:].rearrange("p a r -> p (a r)").bitcast(I32), 0)
        nc.sync.dma_start(offsets[:], offs)
        nc.sync.dma_start(out=wgt_sb[:, 0:WGT_AHEAD], in_=wgt[:, 0:WGT_AHEAD])
        for r in range(4):
            nc.sync.dma_start(
                out=wg_scales_raw[r:P:QUADRANT, :, :].bitcast(I32),
                in_=wg_scales[:, r:16:4, :].rearrange("a q n -> q a n").bitcast(I32),
            )
        for a in range(PASSES):
            rows = xT[a * PASS_K : (a + 1) * PASS_K, :].rearrange("(p i) t -> p i t", i=PACK)
            for i in range(PACK):
                nc.sync.dma_start(out=planes[a][i][:], in_=rows[:, i, :])
                if (a, i) == (0, 0):
                    nc.sync.dma_start(out=wgt_sb[:, WGT_AHEAD:J], in_=wgt[:, WGT_AHEAD:J])
                if (a, i) == (1, 0):
                    nc.sync.dma_start(
                        out=wg_words_raw[:].bitcast(I32),
                        in_=wg_words.rearrange("a p n -> p a n").bitcast(I32),
                    )
        for a in range(PASSES):
            rows = wu[a * PASS_K : (a + 1) * PASS_K, :].rearrange("(p i) r -> p i r", i=PACK)
            nc.sync.dma_start(out=wu_raw[a][:], in_=rows)
        nc.sync.dma_start(out=wd_raw, in_=wd.rearrange("(p i) n -> p i n", i=PACK))
        with nc.allow_non_contiguous_dma(reason="one bias value for each partition and result"):
            nc.sync.dma_start(out=bias[:], in_=b.rearrange("(t p) -> p t", t=PACK))

        nc.vector.tensor_copy(
            out=wg_scale[:],
            in_=wg_scales_raw[:].rearrange("p a (m t) -> p a t m", t=PACK),
        )

        xg_first = tile("xg_first", [P, PACK, J], F32)
        xg = [
            [xg_first[:, :, half * HALF : (half + 1) * HALF] for half in range(2)],
            [shared[:, 2 : PACK + 2, 0:HALF], shared[:, 0:PACK, 0:HALF]],
        ]
        wu_bf16 = [tile("wu_bf16_%d" % a, [P, PACK, P, PACK], BF16)[:] for a in range(PASSES)]
        wd_start = (PACK + 2) * HALF - 2 * WD_SPLIT
        after_wu = tile("after_wu", [P, wd_start + 2 * N], F32, tag="wu_raw1")
        xg_last = after_wu[:, PACK * HALF : (PACK + 2) * HALF].bitcast(BF16)
        xg_bf16 = [
            [tile("xg_bf16_0%d" % half, [P, HALF, PACK], BF16)[:] for half in range(2)],
            [tile("xg_bf16_10", [P, HALF, PACK], BF16)[:], xg_last.rearrange("p (j i) -> p j i", i=PACK)],
        ]
        xg_codes = [tile("xg_codes%d" % a, [P, J], U32) for a in range(PASSES)]
        xg_scale = [tile("xg_scale%d" % a, [P, J], U8) for a in range(PASSES)]

        def gather(a, i, j0, width):
            half, c0 = divmod(j0, HALF)
            nc.vector.tensor_tensor(
                xg_first[:, i, j0 : j0 + width] if a == 0 else xg[a][half][:, i, c0 : c0 + width],
                planes[a][i][:].indirect(offsets[:, j0 // LIST_ROWS : (j0 + width) // LIST_ROWS]),
                wgt_sb[:, j0 : j0 + width],
                MULT,
            )

        def activation_copy(out, in_):
            nc.scalar.activation(out=out, in_=in_, func=ACT.Copy)

        def interleave_xg(copy, a, j0, width):
            half, c0 = divmod(j0, HALF)
            copy(
                out=xg_bf16[a][half][:, c0 : c0 + width, :].rearrange("p (c e) i -> p c i e", e=RUN),
                in_=xg[a][half][:, :, c0 : c0 + width].rearrange("p i (c e) -> p c i e", e=RUN),
            )

        def quantize(codes, scale, src):
            nc.vector.quantize_mx(out=codes.bitcast(FP8X4), scales=scale, in_=src)

        def quantize_xg(a, j0, width):
            half, c0 = divmod(j0, HALF)
            cols = slice(j0, j0 + width)
            src = xg_bf16[a][half][:, c0 : c0 + width, :].rearrange("p j i -> p (j i)")
            quantize(xg_codes[a][:, cols], xg_scale[a][:, cols], src)

        def interleave_weight(copy, raw, dst, m0, m1):
            copy(
                out=dst.rearrange("p t m i -> p m i t")[:, m0:m1],
                in_=raw.rearrange("p i (m t) -> p m i t", t=PACK)[:, m0:m1],
            )

        wu_codes = [tile("wu_codes%d" % a, [P, R], U32) for a in range(PASSES)]
        wu_scale = [tile("wu_scale%d" % a, [P, R], U8) for a in range(PASSES)]
        wd_bf16 = after_wu[:, wd_start:].bitcast(BF16)

        def quantize_wu(a):
            quantize(wu_codes[a][:], wu_scale[a][:], wu_bf16[a].rearrange("p t m i -> p (t m i)"))

        for i in range(PACK):
            if i == 0:
                gather(0, i, 0, WGT_AHEAD)
                gather(0, i, WGT_AHEAD, J - WGT_AHEAD)
            elif i == PACK - 1:
                gather(0, i, 0, HALF)
                gather(0, i, HALF, HALF)
            else:
                gather(0, i, 0, J)
        for half in range(2):
            interleave_xg(activation_copy, 0, half * HALF, HALF)
        nc.scalar.copy(
            out=wg_codes[:].bitcast(U16),
            in_=wg_words_raw[:].bitcast(U16).rearrange("p a (m t) -> p a t m", t=PACK),
        )

        gather(1, 0, 0, HALF)
        gather(1, 0, HALF, HALF)
        gather(1, 1, 0, HALF)
        quantize_xg(0, 0, HALF)
        gather(1, 2, 0, HALF)
        quantize_xg(0, HALF, HALF)
        for j0, width in ((0, FIRST), (FIRST, HALF - FIRST)):
            gather(1, 3, j0, width)
            interleave_xg(nc.scalar.copy, 1, j0, width)

        interleave_weight(nc.scalar.copy, wu_raw[0][:], wu_bf16[0], 0, WU_SPLIT)
        interleave_weight(nc.scalar.copy, wu_raw[1][:], wu_bf16[1], 0, P)
        gather(1, 1, HALF, HALF)
        quantize_xg(1, 0, HALF)
        interleave_weight(nc.vector.tensor_copy, wu_raw[0][:], wu_bf16[0], WU_SPLIT, P)
        gather(1, 2, HALF, HALF)
        gather(1, 3, HALF, HALF)
        quantize_wu(0)
        quantize_wu(1)
        for quarter in range(2, 4):
            interleave_xg(nc.vector.tensor_copy, 1, quarter * QUARTER, QUARTER)
        for quarter in range(2, 4):
            quantize_xg(1, quarter * QUARTER, QUARTER)

        wd_codes = tile("wd_codes", [P, N], U32)
        wd_scale = tile("wd_scale", [P, N], U8)
        tanh_ga = [
            after_wu[:, 0 : PACK * HALF].rearrange("p (t j) -> p t j", t=PACK),
            tile("tanh_ga1", [P, PACK, HALF], F32)[:],
        ]
        h_on_wd = wd_tile[:, 0 : 4 * CHUNK].bitcast(BF16).rearrange("p (j t) -> p j t", t=PACK)
        h_bf16 = [
            h_on_wd if g == 1 else tile("h_bf16_%d" % g, [P, width, PACK], BF16)[:]
            for g, (j0, width) in enumerate(GROUPS)
        ]
        h_codes = [tile("h_codes%d" % g, [P, width], U32) for g, (j0, width) in enumerate(GROUPS)]
        h_scale = [tile("h_scale%d" % g, [P, width], U8) for g, (j0, width) in enumerate(GROUPS)]
        result = [
            [tile("result%d%d" % (g, pair), [P, 2, width], F32) for pair in range(2)]
            for g, (j0, width) in enumerate(GROUPS)
        ]
        out_rows = out.rearrange("(t p) j -> p t j", t=PACK)

        gate_pools = ((0, 0, 0, 2), (1, 1, 1, 1))
        ga = [
            [psum[k].tile([P, HALF], F32, name="ga%d%d" % (half, t), tag="bank") for t, k in enumerate(pools)]
            for half, pools in enumerate(gate_pools)
        ]

        def gate_pass(half, t, a, start):
            cols = slice(half * HALF, (half + 1) * HALF)
            nc.tensor.matmul_mx(
                out=ga[half][t][:],
                lhsT=wg_codes[:, a, t, :].bitcast(FP4X4),
                lhsT_scale=wg_scale[:, a, t, :],
                rhs=xg_codes[a][:, cols].bitcast(FP8X4),
                rhs_scale=xg_scale[a][:, cols],
                start=start,
                stop=not start,
            )

        def gate_tanh(half):
            for t in range(PACK):
                nc.scalar.activation(out=tanh_ga[half][:, t, :], in_=ga[half][t][:], func=ACT.Tanh)

        def up_product(chunk):
            cols = slice(chunk * CHUNK, (chunk + 1) * CHUNK)
            ub = psum[0].tile([P, PACK, CHUNK], F32, name="ub", tag="bank")
            for t in range(PACK):
                for a in range(PASSES):
                    nc.tensor.matmul_mx(
                        out=ub[:, t, :],
                        lhsT=wu_codes[a][:, t * P : (t + 1) * P].bitcast(FP8X4),
                        lhsT_scale=wu_scale[a][:, t * P : (t + 1) * P],
                        rhs=xg_codes[a][:, cols].bitcast(FP8X4),
                        rhs_scale=xg_scale[a][:, cols],
                        start=(a == 0),
                        stop=(a == PASSES - 1),
                    )
            return ub

        def form_h(chunk, ub):
            g = max(k for k, (j0, width) in enumerate(GROUPS) if j0 <= chunk * CHUNK)
            in_group = chunk * CHUNK - GROUPS[g][0]
            half, in_half = divmod(chunk * CHUNK, HALF)
            nc.vector.tensor_tensor(
                h_bf16[g][:, in_group : in_group + CHUNK, :].rearrange("p (c e) t -> p c t e", e=RUN),
                ub[:].rearrange("p t (c e) -> p c t e", e=RUN),
                tanh_ga[half][:, :, in_half : in_half + CHUNK].rearrange("p t (c e) -> p c t e", e=RUN),
                MULT,
            )

        def quantize_h(g):
            quantize(h_codes[g][:], h_scale[g][:], h_bf16[g].rearrange("p j t -> p (j t)"))

        def down_product(g):
            j0, width = GROUPS[g]
            for pair in range(2):
                y = psum[DOWN_POOLS[g][pair]].tile([P, 2, width], F32, name="y", tag="bank")
                for v in range(2):
                    t = 2 * pair + v
                    nc.tensor.matmul_mx(
                        out=y[:, v, :],
                        lhsT=wd_codes[:, t * P : (t + 1) * P].bitcast(FP8X4),
                        lhsT_scale=wd_scale[:, t * P : (t + 1) * P],
                        rhs=h_codes[g][:].bitcast(FP8X4),
                        rhs_scale=h_scale[g][:],
                        start=True,
                        stop=True,
                    )
                if g in VECTOR_EMPTIES and pair == 1:
                    both = bias[:, 2:4].unsqueeze(2).to_broadcast([P, 2, width])
                    nc.vector.tensor_tensor(result[g][pair][:], y[:], both, ADD)
                else:
                    for v in range(2):
                        t = 2 * pair + v
                        dst = result[g][pair][:, v, :]
                        nc.scalar.activation(out=dst, in_=y[:, v, :], func=ACT.Identity, bias=bias[:, t : t + 1])
                nc.sync.dma_start(out=out_rows[:, 2 * pair : 2 * pair + 2, j0 : j0 + width], in_=result[g][pair][:])

        for t in range(PACK):
            gate_pass(1, t, 0, True)
        for t in range(PACK):
            gate_pass(0, t, 1, True)
            gate_pass(0, t, 0, False)
        gate_tanh(0)
        nc.scalar.copy(
            out=wd_bf16.rearrange("p (c e i) -> p c i e", e=RUN, i=PACK)[:, WD_SPLIT // RUN :],
            in_=wd_raw.rearrange("p i (c e) -> p c i e", e=RUN)[:, WD_SPLIT // RUN :],
        )
        nc.gpsimd.tensor_scalar(
            wd_bf16[:, 0 : PACK * WD_SPLIT].rearrange("p (c e i) -> p c i e", e=RUN, i=PACK),
            wd_raw[:, :, 0:WD_SPLIT].rearrange("p i (c e) -> p c i e", e=RUN),
            1.0,
            0.0,
            MULT,
            ADD,
        )

        ub = [up_product(chunk) for chunk in range(3)]
        for t in range(PACK):
            gate_pass(1, t, 1, False)
        gate_tanh(1)
        form_h(0, ub[0])
        ub.append(up_product(3))
        form_h(1, ub[1])
        ub.append(up_product(4))
        form_h(2, ub[2])
        quantize_h(0)
        quantize(wd_codes[:], wd_scale[:], wd_bf16)
        down_product(0)
        ub.append(up_product(5))
        form_h(3, ub[3])
        ub.append(up_product(6))
        form_h(4, ub[4])
        quantize_h(1)
        down_product(1)
        ub.append(up_product(7))
        form_h(5, ub[5])
        quantize_h(2)
        down_product(2)
        form_h(6, ub[6])
        quantize_h(3)
        form_h(7, ub[7])
        quantize_h(4)
        quantize_h(5)
        down_product(3)
        down_product(4)
        down_product(5)
